import numpy as np
import ml_dtypes


def mxq(x, axis, fmt="e4m3"):
    dtype, down = {"e4m3": (ml_dtypes.float8_e4m3fn, 7), "e5m2": (ml_dtypes.float8_e5m2, 14)}[fmt]
    v = np.moveaxis(np.asarray(x, np.float32).astype(ml_dtypes.bfloat16).astype(np.float64), axis, -1)
    blocks = v.reshape(v.shape[:-1] + (-1, 32))
    amax = np.abs(blocks).max(-1, keepdims=True)
    byte = np.maximum(np.where(amax > 0, np.frexp(amax)[1] - 1 + 127, 0) - down, 1)
    scale = np.exp2(byte - 127.0)
    codes = (blocks / scale).astype(np.float32).astype(dtype).astype(np.float64)
    return np.moveaxis((codes * scale).reshape(v.shape), -1, axis)


WIDE = False


def mx_kscale(k):
    if not WIDE:
        return np.ones(k)
    levels = np.array([10, -10, 5, -5, 0])
    if k % 512:
        return np.exp2(np.random.permutation(np.resize(levels, k // 32))).repeat(32)
    a = np.empty((k // 512, 16))
    for p in range(k // 512):
        a[p, :8] = np.random.permutation(np.resize(levels, 8))
        for g in range(8):
            far = levels[np.abs(levels - a[p, g]) >= 10]
            a[p, g + 8] = far[np.random.randint(len(far))]
    return np.exp2(a.ravel()).repeat(32)


def f64(x):
    return np.asarray(x).astype(np.float64)


def striped(idx):
    return np.tile(idx.reshape(-1, 16).T, (8, 1)).astype(np.uint16)


def unstriped(offs):
    return offs[:16].T.reshape(-1).astype(np.int64)


def pack_weight(w):
    k, n = w.shape
    w = f64(np.asarray(w, np.float32).astype(ml_dtypes.bfloat16)).reshape(k // 32, 32, n)
    amax = np.abs(w).max(1)
    byte = np.clip(np.where(amax > 0, np.frexp(amax)[1] - 1 + 127 - 7, 1), 1, 254)
    scaled = (w * np.exp2(127.0 - byte)[:, None, :]).reshape(k, n).astype(np.float32)
    words = np.ascontiguousarray(scaled.reshape(k // 512, 128, 4, n).transpose(0, 1, 3, 2)).astype(ml_dtypes.float8_e4m3fn).view(np.uint8)
    return words, np.ascontiguousarray(byte.astype(np.uint8).reshape(k // 512, 16, n))


def unpack_weight(words, scales):
    g, p, n, _ = words.shape
    vals = np.ascontiguousarray(words).view(ml_dtypes.float8_e4m3fn).astype(np.float64) * np.repeat(np.exp2(scales.astype(np.float64) - 127.0), 8, axis=1)[..., None]
    return vals.transpose(0, 1, 3, 2).reshape(g * 512, n)


def silu(v):
    return v / (1.0 + np.exp(-np.maximum(v, -700.0)))


K, T, S, H, N, U = 1024, 2048, 1024, 512, 256, 1024


def setup_inputs():
    n = np.random.standard_normal
    s = mx_kscale(K)[:, None]
    u = mx_kscale(H)
    packed_xT = pack_weight(n((K, T)) * s)
    return {
        "x_words": packed_xT[0],
        "x_scales": packed_xT[1],
        "w1": (n((K, H)) / np.sqrt(2 * K) / s * u).astype(np.float32),
        "w2": (n((K, H)) / np.sqrt(2 * K) / s * u).astype(np.float32),
        "w3": (n((H, N)) / np.sqrt(H) / u[:, None]).astype(np.float32),
        "offs": striped(np.random.permutation(T)[:S]),
        "src": striped(np.random.permutation(S)[(S * np.random.uniform(0, 1, U) ** 4).astype(np.int64)]),
        "dst": striped(np.random.permutation(S)),
    }


def reference(x_words, x_scales, w1, w2, w3, offs, src, dst):
    xq = unpack_weight(x_words, x_scales)[:, unstriped(offs)]
    y = mxq(f64(w1), 0, "e4m3").T @ xq
    e = mxq(f64(w2), 0, "e4m3").T @ xq
    z = silu(y[:, unstriped(src)] + e[:, unstriped(dst)])
    return mxq(f64(w3), 0, "e4m3").T @ mxq(z, 0, "e4m3")

@@ -1,0 +1,278 @@
+from contextlib import ExitStack
+
+import concourse.mybir as mybir
+from concourse.masks import make_identity
+
+K, T, S, H, N = 1024, 2048, 1024, 512, 256
+FLOPS = 2 * (2 * K * H * S + H * N * S)
+
+F32 = mybir.dt.float32
+BF16 = mybir.dt.bfloat16
+I32 = mybir.dt.int32
+U32 = mybir.dt.uint32
+U16 = mybir.dt.uint16
+U8 = mybir.dt.uint8
+FP8X4 = mybir.dt.float8_e4m3fn_x4
+SILU = mybir.ActivationFunctionType.Silu
+MULT = mybir.AluOpType.mult
+ADD = mybir.AluOpType.add
+
+P = 128
+PACK = 4
+PASSES = K // (P * PACK)
+HALF = 512
+TILES = H // P
+UNITS = [[0,256],[512,768],[256,512],[768,896],[896,1024]]
+X_CUTS = [[0,512],[512,768],[768,1024]]
+OUT_ON_VECTOR = [0,1,3]
+Z_ON_VECTOR = []
+
+
+def tile_picked_hub_silu_p_kernel(
+    tc, x_words, x_scales, w1, w2, w3, offs, src, dst, out
+):
+    nc = tc.nc
+    with ExitStack() as ctx:
+        keep = ctx.enter_context(tc.tile_pool(name="keep", bufs=1))
+        psum = ctx.enter_context(tc.psum_pool(name="psum", bufs=1))
+
+        def held(shape, dtype, name, tag=None):
+            return keep.tile(shape, dtype, name=name, tag=tag or name, align_bytes=64)
+
+        def bank(b, shape, name):
+            return psum.tile(shape, F32, name=name, tag="bank%d" % b)
+
+        def entries(lst, lo, hi):
+            return lst[:, lo // 16 : hi // 16]
+
+        offs_t = held([P, S // 16], U16, "offs_t")
+        src_t = held([P, S // 16], U16, "src_t")
+        dst_t = held([P, S // 16], U16, "dst_t")
+        xw = [held([P, T], U32, "xw%d" % z) for z in range(PASSES)]
+        xs = held([P, T], U8, "xs")
+
+        def load_words(z):
+            nc.sync.dma_start(
+                out=xw[z][:].bitcast(I32),
+                in_=x_words[z].rearrange("p n t -> p (n t)").bitcast(I32),
+            )
+
+        raw = {}
+
+        def load_columns(which, w, c0, c1):
+            passes = w.shape[0] // (P * PACK)
+            tag = "first_row" if (which, c0) == (1, 0) else None
+            t = held([P, passes, PACK, c1 - c0], F32, "raw%d_%d" % (which, c0), tag)
+            for z in range(passes):
+                rows = w[z * P * PACK : (z + 1) * P * PACK, c0:c1]
+                nc.sync.dma_start(out=t[:, z], in_=rows.rearrange("(p j) c -> p j c", j=PACK))
+            if which == 2:
+                raw[(2, 0)] = t[:, 0].rearrange("p j (m c) -> p m j c", c=P)
+            else:
+                for c in range(c0, c1, P):
+                    raw[(which, c // P)] = t[:, :, :, c - c0 : c - c0 + P]
+
+        nc.vector.memset(xs[:].bitcast(I32), 0)
+        nc.sync.dma_start(offs_t[:], offs)
+        load_words(0)
+        for q in range(4):
+            nc.sync.dma_start(
+                out=xs[32 * q : 32 * q + 4 * PASSES, :].bitcast(I32),
+                in_=x_scales[:, 4 * q : 4 * q + 4, :].bitcast(I32),
+            )
+        load_columns(0, w1, 0, P)
+        load_words(1)
+        load_columns(1, w2, 0, P)
+        nc.sync.dma_start(src_t[:], src)
+        nc.sync.dma_start(dst_t[:], dst)
+        load_columns(0, w1, P, 2 * P)
+        load_columns(1, w2, P, 2 * P)
+        load_columns(0, w1, 2 * P, 4 * P)
+        load_columns(1, w2, 2 * P, 4 * P)
+        load_columns(2, w3, 0, N)
+
+        ident = held([P, P], F32, "ident")
+        make_identity(nc, ident[:])
+        warm = held([P, 8], F32, "warm")
+        nc.scalar.activation(warm[:, 0:1], ident[:, 0:1], SILU)
+
+        xg = [held([P, S], U32, "xg%d" % z) for z in range(PASSES)]
+        xsg = held([P, S], U8, "xsg")
+        nc.vector.tensor_copy(xg[0][:], xw[0][:].indirect(offs_t[:]))
+        nc.vector.tensor_copy(xsg[:], xs[:].indirect(offs_t[:]))
+
+        codes = {}
+
+        def weave(grouped, rows):
+            return (
+                grouped.rearrange("p a (c i j) -> p a c j i", i=4, j=PACK),
+                rows.rearrange("p a j (c i) -> p a c j i", i=4),
+            )
+
+        def on_scalar(grouped, rows):
+            nc.scalar.copy(*weave(grouped, rows))
+
+        def on_scalar_apart(grouped, rows):
+            woven, plain = weave(grouped, rows)
+            for a in range(2):
+                nc.scalar.copy(woven[:, a], plain[:, a])
+
+        def on_vector(grouped, rows):
+            nc.vector.tensor_copy(*weave(grouped, rows))
+
+        def on_gpsimd(grouped, rows):
+            woven, plain = weave(grouped, rows)
+            for a in range(2):
+                nc.gpsimd.tensor_scalar(woven[:, a], plain[:, a], 1.0, 0.0, MULT, ADD)
+
+        def prepare(cast, key):
+            name = "%d_%d" % key
+            grouped = held([P, 2, P * PACK], BF16, "g" + name)
+            cast(grouped[:], raw[key])
+            words = held([P, 2, P], U32, "c" + name)
+            scales = held([P, 2, P], U8, "s" + name)
+            nc.vector.quantize_mx(
+                out=words[:].rearrange("p a c -> p (a c)").bitcast(FP8X4),
+                scales=scales[:].rearrange("p a c -> p (a c)"),
+                in_=grouped[:].rearrange("p a c -> p (a c)"),
+            )
+            codes[key] = (words, scales)
+
+        steps = [(which, t) for t in range(TILES) for which in range(2)]
+        casts = [on_scalar_apart, on_scalar, on_vector, on_scalar, on_scalar, on_scalar, on_scalar, on_scalar]
+
+        prepare(casts[0], steps[0])
+        for lo, hi in X_CUTS:
+            nc.vector.tensor_copy(xg[1][:, lo:hi], xw[1][:].indirect(entries(offs_t, lo, hi)))
+        prepare(casts[1], steps[1])
+
+        lists = (src_t, dst_t)
+        zt = [held([P, HALF // P, H], BF16, "zt%d" % h) for h in range(2)]
+        rows = {}
+        picked = {}
+
+        def product(n):
+            words, scales = codes[steps[n]]
+            cuts = X_CUTS if n == 0 else [(0, HALF), (HALF, S)]
+            acc = [bank((2 * n + h) % 4 if h < 2 else 4, [P, hi - lo], "acc%d_%d" % (n, h)) for h, (lo, hi) in enumerate(cuts)]
+            for z in range(PASSES):
+                for h, (lo, hi) in enumerate(cuts):
+                    nc.tensor.matmul_mx(
+                        out=acc[h][:],
+                        lhsT=words[:, z, :].bitcast(FP8X4),
+                        lhsT_scale=scales[:, z, :],
+                        rhs=xg[z][:, lo:hi].bitcast(FP8X4),
+                        rhs_scale=xsg[4 * z : P, lo:hi],
+                        start=(z == 0),
+                        stop=(z == PASSES - 1),
+                    )
+            rows[n] = held([P, S], F32, "row%d" % n, "first_row" if n == 0 else None)
+            for h, (lo, hi) in enumerate(cuts):
+                nc.scalar.copy(rows[n][:, lo:hi], acc[h][:])
+
+        def fetch(n, into, lo, hi):
+            nc.vector.tensor_copy(into, rows[n][:].indirect(entries(lists[n % 2], lo, hi)))
+
+        def add_turned(pre, a, b, blocks):
+            for k, part in enumerate((a, b)):
+                for blk in range(blocks):
+                    nc.tensor.matmul(
+                        pre[:, blk, :], part[:, blk * P : (blk + 1) * P], ident[:],
+                        start=(k == 0 and blk == 0), stop=(k == 1 and blk == blocks - 1),
+                        is_transpose=True,
+                    )
+
+        def hidden_tile(t):
+            for h in range(2):
+                pre = bank(3 if (t, h) == (TILES - 2, 1) else 4 + h, [P, HALF // P, P], "pre%d_%d" % (t, h))
+                cols = slice(h * HALF, (h + 1) * HALF)
+                add_turned(pre, picked[2 * t][:, cols], picked[2 * t + 1][:, cols], HALF // P)
+                nc.scalar.activation(zt[h][:, :, t * P : (t + 1) * P], pre[:], SILU)
+
+        last = TILES - 1
+        for n in range(len(steps)):
+            if n + 2 < len(steps):
+                prepare(casts[n + 2], steps[n + 2])
+            product(n)
+            if n == 3:
+                prepare(on_gpsimd, (2, 0))
+            if n >= 3 and (n - 3) % 2 == 0:
+                hidden_tile((n - 3) // 2)
+            if n // 2 < last:
+                picked[n] = held([P, S], F32, "picked%d" % n)
+                for h in range(2):
+                    fetch(n, picked[n][:, h * HALF : (h + 1) * HALF], h * HALF, (h + 1) * HALF)
+
+        first = UNITS[0][1] - UNITS[0][0]
+        head = held([P, 2, first], F32, "head")
+        rest = held([P, 2, S - first], F32, "rest", "picked%d" % (2 * last - 2))
+        parts = []
+        at = 0
+        for u, (lo, hi) in enumerate(UNITS):
+            part = head[:] if u == 0 else rest[:, :, at : at + hi - lo]
+            at = at + (hi - lo if u else 0)
+            parts.append(part)
+            for which in range(2):
+                fetch(2 * last + which, part[:, which, :], lo, hi)
+
+        taken = []
+
+        def next_bank(shape, name):
+            taken.append(name)
+            return bank(4 + (len(taken) - 1) % 3, shape, name)
+
+        def finish(u):
+            z_in = z_ins[u]
+            lo, hi = UNITS[u]
+            width = hi - lo
+            words = held([P, width], U32, "zc%d" % u)
+            scales = held([P, width], U8, "zs%d" % u)
+            nc.vector.quantize_mx(out=words[:].bitcast(FP8X4), scales=scales[:], in_=z_in[:])
+            acc = bank(u % 3, [P, N // P, width], "oacc%d" % u)
+            w_words, w_scales = codes[(2, 0)]
+            for m in range(N // P):
+                nc.tensor.matmul_mx(
+                    out=acc[:, m, :],
+                    lhsT=w_words[:, m, :].bitcast(FP8X4),
+                    lhsT_scale=w_scales[:, m, :],
+                    rhs=words[:].bitcast(FP8X4),
+                    rhs_scale=scales[:],
+                    start=True,
+                    stop=True,
+                )
+            result = held([P, N // P, width], F32, "res%d" % u)
+            copy_out = nc.vector.tensor_copy if u in OUT_ON_VECTOR else nc.scalar.copy
+            copy_out(result[:], acc[:])
+            nc.sync.dma_start(out=out[:, lo:hi].rearrange("(m p) r -> p m r", p=P), in_=result[:])
+
+        z_ins = {}
+
+        def rows_of(u):
+            lo, hi = UNITS[u]
+            b0 = (lo % HALF) // P
+            return zt[lo // HALF][:, b0 : b0 + (hi - lo) // P, :]
+
+        def activate(u):
+            blocks = (UNITS[u][1] - UNITS[u][0]) // P
+            pre = next_bank([P, blocks, P], "pre_last%d" % u)
+            add_turned(pre, parts[u][:, 0, :], parts[u][:, 1, :], blocks)
+            nc.scalar.activation(rows_of(u)[:, :, last * P : H], pre[:], SILU)
+
+        def turn_back(u):
+            blocks = (UNITS[u][1] - UNITS[u][0]) // P
+            turned = next_bank([P, blocks, 2, P], "turned%d" % u)
+            pairs = rows_of(u).bitcast(F32)
+            for blk in range(blocks):
+                for v in range(2):
+                    nc.tensor.transpose(turned[:, blk, v, :], pairs[:, blk, v : 2 * P : 2], ident[:])
+            z_ins[u] = held([P, blocks * P * PACK], BF16, "z_in%d" % u)
+            copy_z = nc.vector.tensor_copy if u in Z_ON_VECTOR else nc.scalar.copy
+            copy_z(
+                z_ins[u][:].bitcast(F32).rearrange("p (b r v) -> p b r v", b=blocks, v=2),
+                turned[:].rearrange("p b v r -> p b r v"),
+            )
+
+        for s in range(len(UNITS) + 3):
+            for stage, behind in ((activate, 0), (turn_back, 1), (finish, 3)):
+                if 0 <= s - behind < len(UNITS):
+                    stage(s - behind)

@@ -1,7 +1,6 @@
 from contextlib import ExitStack
 
 import concourse.mybir as mybir
-from concourse.masks import make_identity
 
 K, T, S, H, N = 1024, 2048, 1024, 512, 256
 FLOPS = 2 * (2 * K * H * S + H * N * S)
@@ -14,7 +13,6 @@ U16 = mybir.dt.uint16
 U8 = mybir.dt.uint8
 FP8X4 = mybir.dt.float8_e4m3fn_x4
 SILU = mybir.ActivationFunctionType.Silu
-MULT = mybir.AluOpType.mult
 ADD = mybir.AluOpType.add
 
 P = 128
@@ -22,10 +20,8 @@ PACK = 4
 PASSES = K // (P * PACK)
 HALF = 512
 TILES = H // P
-UNITS = [[0,256],[512,768],[256,512],[768,896],[896,1024]]
-X_CUTS = [[0,512],[512,768],[768,1024]]
-OUT_ON_VECTOR = [0,1,3]
-Z_ON_VECTOR = []
+RUN = 4
+SPANS = [(0, 256), (256, 512), (512, 768), (768, 896), (896, 1024)]
 
 
 def tile_picked_hub_silu_p_kernel(
@@ -59,18 +55,10 @@ def tile_picked_hub_silu_p_kernel(
 
         raw = {}
 
-        def load_columns(which, w, c0, c1):
-            passes = w.shape[0] // (P * PACK)
-            tag = "first_row" if (which, c0) == (1, 0) else None
-            t = held([P, passes, PACK, c1 - c0], F32, "raw%d_%d" % (which, c0), tag)
-            for z in range(passes):
-                rows = w[z * P * PACK : (z + 1) * P * PACK, c0:c1]
-                nc.sync.dma_start(out=t[:, z], in_=rows.rearrange("(p j) c -> p j c", j=PACK))
-            if which == 2:
-                raw[(2, 0)] = t[:, 0].rearrange("p j (m c) -> p m j c", c=P)
-            else:
-                for c in range(c0, c1, P):
-                    raw[(which, c // P)] = t[:, :, :, c - c0 : c - c0 + P]
+        def load_pass(which, w, z):
+            raw[(which, z)] = held([P, PACK, H], F32, "raw%d_%d" % (which, z))
+            rows = w[z * P * PACK : (z + 1) * P * PACK, :]
+            nc.sync.dma_start(out=raw[(which, z)][:], in_=rows.rearrange("(p j) c -> p j c", j=PACK))
 
         nc.vector.memset(xs[:].bitcast(I32), 0)
         nc.sync.dma_start(offs_t[:], offs)
@@ -80,199 +68,211 @@ def tile_picked_hub_silu_p_kernel(
                 out=xs[32 * q : 32 * q + 4 * PASSES, :].bitcast(I32),
                 in_=x_scales[:, 4 * q : 4 * q + 4, :].bitcast(I32),
             )
-        load_columns(0, w1, 0, P)
+        load_pass(0, w1, 0)
         load_words(1)
-        load_columns(1, w2, 0, P)
+        load_pass(0, w1, 1)
         nc.sync.dma_start(src_t[:], src)
+        load_pass(1, w2, 0)
         nc.sync.dma_start(dst_t[:], dst)
-        load_columns(0, w1, P, 2 * P)
-        load_columns(1, w2, P, 2 * P)
-        load_columns(0, w1, 2 * P, 4 * P)
-        load_columns(1, w2, 2 * P, 4 * P)
-        load_columns(2, w3, 0, N)
+        load_pass(1, w2, 1)
+        raw3 = held([P, TILES, N], F32, "raw3")
+        w3_rows = w3.rearrange("(c t i) m -> t c i m", t=TILES, i=RUN)
+        for t in range(TILES):
+            nc.sync.dma_start(out=raw3[:, t, :], in_=w3_rows[t])
 
-        ident = held([P, P], F32, "ident")
-        make_identity(nc, ident[:])
-        warm = held([P, 8], F32, "warm")
-        nc.scalar.activation(warm[:, 0:1], ident[:, 0:1], SILU)
+        warm = held([P, 16], F32, "warm")
+        nc.vector.memset(warm[:, 0:8], 0.0)
+        nc.scalar.activation(warm[:, 8:9], warm[:, 0:1], SILU)
 
-        xg = [held([P, S], U32, "xg%d" % z) for z in range(PASSES)]
-        xsg = held([P, S], U8, "xsg")
-        nc.vector.tensor_copy(xg[0][:], xw[0][:].indirect(offs_t[:]))
-        nc.vector.tensor_copy(xsg[:], xs[:].indirect(offs_t[:]))
+        on_scalar = nc.scalar.copy
+        on_vector = nc.vector.tensor_copy
 
-        codes = {}
-
-        def weave(grouped, rows):
-            return (
-                grouped.rearrange("p a (c i j) -> p a c j i", i=4, j=PACK),
-                rows.rearrange("p a j (c i) -> p a c j i", i=4),
-            )
-
-        def on_scalar(grouped, rows):
-            nc.scalar.copy(*weave(grouped, rows))
-
-        def on_scalar_apart(grouped, rows):
-            woven, plain = weave(grouped, rows)
-            for a in range(2):
-                nc.scalar.copy(woven[:, a], plain[:, a])
-
-        def on_vector(grouped, rows):
-            nc.vector.tensor_copy(*weave(grouped, rows))
-
-        def on_gpsimd(grouped, rows):
-            woven, plain = weave(grouped, rows)
-            for a in range(2):
-                nc.gpsimd.tensor_scalar(woven[:, a], plain[:, a], 1.0, 0.0, MULT, ADD)
-
-        def prepare(cast, key):
-            name = "%d_%d" % key
-            grouped = held([P, 2, P * PACK], BF16, "g" + name)
-            cast(grouped[:], raw[key])
-            words = held([P, 2, P], U32, "c" + name)
-            scales = held([P, 2, P], U8, "s" + name)
+        def quantise(grouped, count, name):
+            words = held([P, count, P], U32, "c" + name)
+            scales = held([P, count, P], U8, "s" + name)
             nc.vector.quantize_mx(
                 out=words[:].rearrange("p a c -> p (a c)").bitcast(FP8X4),
                 scales=scales[:].rearrange("p a c -> p (a c)"),
                 in_=grouped[:].rearrange("p a c -> p (a c)"),
             )
-            codes[key] = (words, scales)
+            return words, scales
 
-        steps = [(which, t) for t in range(TILES) for which in range(2)]
-        casts = [on_scalar_apart, on_scalar, on_vector, on_scalar, on_scalar, on_scalar, on_scalar, on_scalar]
+        woven = {}
+        codes = {}
 
-        prepare(casts[0], steps[0])
-        for lo, hi in X_CUTS:
-            nc.vector.tensor_copy(xg[1][:, lo:hi], xw[1][:].indirect(entries(offs_t, lo, hi)))
-        prepare(casts[1], steps[1])
+        def cast(copy, which, z, t0, t1):
+            grouped = held([P, t1 - t0, P * PACK], BF16, "g%d_%d_%d" % (which, z, t0))
+            copy(
+                grouped[:].rearrange("p t (c i j) -> p t c j i", i=RUN, j=PACK),
+                raw[(which, z)][:].rearrange("p j (c t i) -> p t c j i", t=TILES, i=RUN)[:, t0:t1],
+            )
+            woven[(which, z, t0)] = (grouped, t1 - t0)
 
-        lists = (src_t, dst_t)
-        zt = [held([P, HALF // P, H], BF16, "zt%d" % h) for h in range(2)]
+        def pack(which, z, t0):
+            grouped, count = woven[(which, z, t0)]
+            words, scales = quantise(grouped, count, "%d_%d_%d" % (which, z, t0))
+            for a in range(count):
+                codes[(which, z, t0 + a)] = (words[:, a, :], scales[:, a, :])
+
+        xg = [held([P, S], U32, "xg0")]
+        xsg = held([P, S], U8, "xsg")
+        acc = {}
         rows = {}
+
+        def multiply(which, z, t):
+            words, scales = codes[(which, z, t)]
+            for h in range(2):
+                if z == 0:
+                    acc[(which, t, h)] = bank(2 * t + h, [P, HALF], "acc%d_%d_%d" % (which, t, h))
+                cols = slice(h * HALF, (h + 1) * HALF)
+                nc.tensor.matmul_mx(
+                    out=acc[(which, t, h)][:],
+                    lhsT=words.bitcast(FP8X4),
+                    lhsT_scale=scales,
+                    rhs=xg[z][:, cols].bitcast(FP8X4),
+                    rhs_scale=xsg[4 * z : P, cols],
+                    start=(z == 0),
+                    stop=(z == PASSES - 1),
+                )
+
+        def empty(which, t, copies=(on_scalar, on_scalar)):
+            rows[(which, t)] = held([P, S], F32, "row%d_%d" % (which, t))
+            for h in range(2):
+                copies[h](rows[(which, t)][:, h * HALF : (h + 1) * HALF], acc[(which, t, h)][:])
+
         picked = {}
 
-        def product(n):
-            words, scales = codes[steps[n]]
-            cuts = X_CUTS if n == 0 else [(0, HALF), (HALF, S)]
-            acc = [bank((2 * n + h) % 4 if h < 2 else 4, [P, hi - lo], "acc%d_%d" % (n, h)) for h, (lo, hi) in enumerate(cuts)]
-            for z in range(PASSES):
-                for h, (lo, hi) in enumerate(cuts):
-                    nc.tensor.matmul_mx(
-                        out=acc[h][:],
-                        lhsT=words[:, z, :].bitcast(FP8X4),
-                        lhsT_scale=scales[:, z, :],
-                        rhs=xg[z][:, lo:hi].bitcast(FP8X4),
-                        rhs_scale=xsg[4 * z : P, lo:hi],
-                        start=(z == 0),
-                        stop=(z == PASSES - 1),
-                    )
-            rows[n] = held([P, S], F32, "row%d" % n, "first_row" if n == 0 else None)
-            for h, (lo, hi) in enumerate(cuts):
-                nc.scalar.copy(rows[n][:, lo:hi], acc[h][:])
-
-        def fetch(n, into, lo, hi):
-            nc.vector.tensor_copy(into, rows[n][:].indirect(entries(lists[n % 2], lo, hi)))
-
-        def add_turned(pre, a, b, blocks):
-            for k, part in enumerate((a, b)):
-                for blk in range(blocks):
-                    nc.tensor.matmul(
-                        pre[:, blk, :], part[:, blk * P : (blk + 1) * P], ident[:],
-                        start=(k == 0 and blk == 0), stop=(k == 1 and blk == blocks - 1),
-                        is_transpose=True,
-                    )
-
-        def hidden_tile(t):
+        def fetch_sources(t):
             for h in range(2):
-                pre = bank(3 if (t, h) == (TILES - 2, 1) else 4 + h, [P, HALF // P, P], "pre%d_%d" % (t, h))
-                cols = slice(h * HALF, (h + 1) * HALF)
-                add_turned(pre, picked[2 * t][:, cols], picked[2 * t + 1][:, cols], HALF // P)
-                nc.scalar.activation(zt[h][:, :, t * P : (t + 1) * P], pre[:], SILU)
+                picked[(t, h)] = held([P, HALF], F32, "picked%d_%d" % (t, h))
+                nc.vector.tensor_copy(
+                    picked[(t, h)][:], rows[(0, t)][:].indirect(entries(src_t, h * HALF, (h + 1) * HALF))
+                )
 
-        last = TILES - 1
-        for n in range(len(steps)):
-            if n + 2 < len(steps):
-                prepare(casts[n + 2], steps[n + 2])
-            product(n)
-            if n == 3:
-                prepare(on_gpsimd, (2, 0))
-            if n >= 3 and (n - 3) % 2 == 0:
-                hidden_tile((n - 3) // 2)
-            if n // 2 < last:
-                picked[n] = held([P, S], F32, "picked%d" % n)
-                for h in range(2):
-                    fetch(n, picked[n][:, h * HALF : (h + 1) * HALF], h * HALF, (h + 1) * HALF)
+        nc.vector.tensor_copy(xg[0][:], xw[0][:].indirect(offs_t[:]))
+        nc.vector.tensor_copy(xsg[:], xs[:].indirect(offs_t[:]))
+        cast(on_scalar, 0, 0, 0, 2)
+        cast(on_scalar, 0, 0, 2, 4)
+        pack(0, 0, 0)
+        multiply(0, 0, 0)
+        multiply(0, 0, 1)
+        xg.append(held([P, S], U32, "xg1", "xs"))
+        nc.vector.tensor_copy(xg[1][:, 0:HALF], xw[1][:].indirect(entries(offs_t, 0, HALF)))
+        pack(0, 0, 2)
+        nc.vector.tensor_copy(xg[1][:, HALF:S], xw[1][:].indirect(entries(offs_t, HALF, S)))
+        cast(on_vector, 0, 1, 0, 1)
+        cast(on_scalar, 0, 1, 1, 2)
+        cast(on_scalar, 0, 1, 2, 3)
+        cast(on_vector, 0, 1, 3, 4)
+        pack(0, 1, 0)
+        multiply(0, 1, 0)
+        pack(0, 1, 1)
+        multiply(0, 1, 1)
+        for t in range(2, TILES):
+            pack(0, 1, t)
+            multiply(0, 0, t)
+            multiply(0, 1, t)
+        empty(0, 0, (on_scalar, on_vector))
+        fetch_sources(0)
+        empty(0, 1)
+        fetch_sources(1)
+        cast(on_scalar, 1, 0, 0, 2)
+        cast(on_scalar, 1, 1, 0, 2)
+        pack(1, 0, 0)
+        pack(1, 1, 0)
+        for t in range(2):
+            for z in range(PASSES):
+                multiply(1, z, t)
+        empty(0, 2)
+        fetch_sources(2)
+        cast(on_scalar, 1, 0, 2, 4)
+        pack(1, 0, 2)
+        empty(0, 3)
+        cast(on_scalar, 1, 1, 2, 4)
+        pack(1, 1, 2)
+        fetch_sources(3)
+        for t in range(2, TILES):
+            for z in range(PASSES):
+                multiply(1, z, t)
+        for t in range(TILES):
+            empty(1, t)
+        grouped3 = held([P, N // P, P * PACK], BF16, "g3")
+        on_scalar(
+            grouped3[:].rearrange("p a (c i j) -> p a c j i", i=RUN, j=PACK),
+            raw3[:].rearrange("p j (a c i) -> p a c j i", a=N // P, i=RUN),
+        )
 
-        first = UNITS[0][1] - UNITS[0][0]
-        head = held([P, 2, first], F32, "head")
-        rest = held([P, 2, S - first], F32, "rest", "picked%d" % (2 * last - 2))
-        parts = []
-        at = 0
-        for u, (lo, hi) in enumerate(UNITS):
-            part = head[:] if u == 0 else rest[:, :, at : at + hi - lo]
-            at = at + (hi - lo if u else 0)
-            parts.append(part)
-            for which in range(2):
-                fetch(2 * last + which, part[:, which, :], lo, hi)
+        sums = {}
+        z_in = {}
+        behind = {2: "picked3_0", 3: "z_in0", 4: "z_in1"}
 
-        taken = []
+        def add_targets(u, t):
+            lo, hi = SPANS[u]
+            if t == 0:
+                sums[u] = held([P, TILES, hi - lo], F32, "sums%d" % u, behind.get(u))
+            nc.vector.tensor_tensor(
+                sums[u][:, t, :],
+                rows[(1, t)][:].indirect(entries(dst_t, lo, hi)),
+                picked[(t, lo // HALF)][:, lo % HALF : lo % HALF + hi - lo],
+                ADD,
+            )
 
-        def next_bank(shape, name):
-            taken.append(name)
-            return bank(4 + (len(taken) - 1) % 3, shape, name)
+        def activate(u):
+            lo, hi = SPANS[u]
+            z_in[u] = held([P, (hi - lo) * PACK], BF16, "z_in%d" % u)
+            nc.scalar.activation(
+                z_in[u][:].rearrange("p (c i t) -> p c t i", i=RUN, t=TILES),
+                sums[u][:].rearrange("p t (c i) -> p c t i", i=RUN),
+                SILU,
+            )
 
-        def finish(u):
-            z_in = z_ins[u]
-            lo, hi = UNITS[u]
-            width = hi - lo
-            words = held([P, width], U32, "zc%d" % u)
-            scales = held([P, width], U8, "zs%d" % u)
-            nc.vector.quantize_mx(out=words[:].bitcast(FP8X4), scales=scales[:], in_=z_in[:])
-            acc = bank(u % 3, [P, N // P, width], "oacc%d" % u)
-            w_words, w_scales = codes[(2, 0)]
+        outs = {}
+
+        def second_layer(u):
+            lo, hi = SPANS[u]
+            words = held([P, hi - lo], U32, "zc%d" % u)
+            scales = held([P, hi - lo], U8, "zs%d" % u)
+            nc.vector.quantize_mx(out=words[:].bitcast(FP8X4), scales=scales[:], in_=z_in[u][:])
+            outs[u] = bank(u, [P, N // P, hi - lo], "oacc%d" % u)
             for m in range(N // P):
                 nc.tensor.matmul_mx(
-                    out=acc[:, m, :],
-                    lhsT=w_words[:, m, :].bitcast(FP8X4),
-                    lhsT_scale=w_scales[:, m, :],
+                    out=outs[u][:, m, :],
+                    lhsT=words3[:, m, :].bitcast(FP8X4),
+                    lhsT_scale=scales3[:, m, :],
                     rhs=words[:].bitcast(FP8X4),
                     rhs_scale=scales[:],
                     start=True,
                     stop=True,
                 )
-            result = held([P, N // P, width], F32, "res%d" % u)
-            copy_out = nc.vector.tensor_copy if u in OUT_ON_VECTOR else nc.scalar.copy
-            copy_out(result[:], acc[:])
+
+        def store(u, copy):
+            lo, hi = SPANS[u]
+            result = held([P, N // P, hi - lo], F32, "res%d" % u)
+            copy(result[:], outs[u][:])
             nc.sync.dma_start(out=out[:, lo:hi].rearrange("(m p) r -> p m r", p=P), in_=result[:])
 
-        z_ins = {}
-
-        def rows_of(u):
-            lo, hi = UNITS[u]
-            b0 = (lo % HALF) // P
-            return zt[lo // HALF][:, b0 : b0 + (hi - lo) // P, :]
-
-        def activate(u):
-            blocks = (UNITS[u][1] - UNITS[u][0]) // P
-            pre = next_bank([P, blocks, P], "pre_last%d" % u)
-            add_turned(pre, parts[u][:, 0, :], parts[u][:, 1, :], blocks)
-            nc.scalar.activation(rows_of(u)[:, :, last * P : H], pre[:], SILU)
-
-        def turn_back(u):
-            blocks = (UNITS[u][1] - UNITS[u][0]) // P
-            turned = next_bank([P, blocks, 2, P], "turned%d" % u)
-            pairs = rows_of(u).bitcast(F32)
-            for blk in range(blocks):
-                for v in range(2):
-                    nc.tensor.transpose(turned[:, blk, v, :], pairs[:, blk, v : 2 * P : 2], ident[:])
-            z_ins[u] = held([P, blocks * P * PACK], BF16, "z_in%d" % u)
-            copy_z = nc.vector.tensor_copy if u in Z_ON_VECTOR else nc.scalar.copy
-            copy_z(
-                z_ins[u][:].bitcast(F32).rearrange("p (b r v) -> p b r v", b=blocks, v=2),
-                turned[:].rearrange("p b v r -> p b r v"),
-            )
-
-        for s in range(len(UNITS) + 3):
-            for stage, behind in ((activate, 0), (turn_back, 1), (finish, 3)):
-                if 0 <= s - behind < len(UNITS):
-                    stage(s - behind)
+        for t in range(TILES):
+            for u in range(2):
+                add_targets(u, t)
+        words3, scales3 = quantise(grouped3, N // P, "3")
+        activate(0)
+        activate(1)
+        for t in range(TILES):
+            add_targets(2, t)
+        second_layer(0)
+        activate(2)
+        store(0, on_scalar)
+        for t in range(TILES):
+            add_targets(3, t)
+        second_layer(1)
+        activate(3)
+        store(1, on_scalar)
+        for t in range(TILES):
+            add_targets(4, t)
+        activate(4)
+        second_layer(2)
+        second_layer(3)
+        store(2, on_scalar)
+        second_layer(4)
+        store(3, on_vector)
+        store(4, on_scalar)

@@ -21,7 +21,7 @@ PASSES = K // (P * PACK)
 HALF = 512
 TILES = H // P
 RUN = 4
-SPANS = [(0, 256), (256, 512), (512, 768), (768, 896), (896, 1024)]
+SPANS = [(0, 256), (256, 512), (512, 768), (768, 896), (896, 960), (960, 1024)]
 
 
 def tile_picked_hub_silu_p_kernel(
@@ -61,8 +61,8 @@ def tile_picked_hub_silu_p_kernel(
             nc.sync.dma_start(out=raw[(which, z)][:], in_=rows.rearrange("(p j) c -> p j c", j=PACK))
 
         nc.vector.memset(xs[:].bitcast(I32), 0)
-        nc.sync.dma_start(offs_t[:], offs)
         load_words(0)
+        nc.sync.dma_start(offs_t[:], offs)
         for q in range(4):
             nc.sync.dma_start(
                 out=xs[32 * q : 32 * q + 4 * PASSES, :].bitcast(I32),
@@ -87,8 +87,8 @@ def tile_picked_hub_silu_p_kernel(
         on_scalar = nc.scalar.copy
         on_vector = nc.vector.tensor_copy
 
-        def quantise(grouped, count, name):
-            words = held([P, count, P], U32, "c" + name)
+        def quantise(grouped, count, name, tag=None):
+            words = held([P, count, P], U32, "c" + name, tag)
             scales = held([P, count, P], U8, "s" + name)
             nc.vector.quantize_mx(
                 out=words[:].rearrange("p a c -> p (a c)").bitcast(FP8X4),
@@ -108,9 +108,9 @@ def tile_picked_hub_silu_p_kernel(
             )
             woven[(which, z, t0)] = (grouped, t1 - t0)
 
-        def pack(which, z, t0):
+        def pack(which, z, t0, tag=None):
             grouped, count = woven[(which, z, t0)]
-            words, scales = quantise(grouped, count, "%d_%d_%d" % (which, z, t0))
+            words, scales = quantise(grouped, count, "%d_%d_%d" % (which, z, t0), tag)
             for a in range(count):
                 codes[(which, z, t0 + a)] = (words[:, a, :], scales[:, a, :])
 
@@ -135,16 +135,16 @@ def tile_picked_hub_silu_p_kernel(
                     stop=(z == PASSES - 1),
                 )
 
-        def empty(which, t, copies=(on_scalar, on_scalar)):
-            rows[(which, t)] = held([P, S], F32, "row%d_%d" % (which, t))
+        def empty(which, t, copies=(on_scalar, on_scalar), tag=None):
+            rows[(which, t)] = held([P, S], F32, "row%d_%d" % (which, t), tag)
             for h in range(2):
                 copies[h](rows[(which, t)][:, h * HALF : (h + 1) * HALF], acc[(which, t, h)][:])
 
         picked = {}
 
-        def fetch_sources(t):
+        def fetch_sources(t, tags=(None, None)):
             for h in range(2):
-                picked[(t, h)] = held([P, HALF], F32, "picked%d_%d" % (t, h))
+                picked[(t, h)] = held([P, HALF], F32, "picked%d_%d" % (t, h), tags[h])
                 nc.vector.tensor_copy(
                     picked[(t, h)][:], rows[(0, t)][:].indirect(entries(src_t, h * HALF, (h + 1) * HALF))
                 )
@@ -157,15 +157,13 @@ def tile_picked_hub_silu_p_kernel(
         multiply(0, 0, 0)
         multiply(0, 0, 1)
         xg.append(held([P, S], U32, "xg1", "xs"))
-        nc.vector.tensor_copy(xg[1][:, 0:HALF], xw[1][:].indirect(entries(offs_t, 0, HALF)))
-        pack(0, 0, 2)
-        nc.vector.tensor_copy(xg[1][:, HALF:S], xw[1][:].indirect(entries(offs_t, HALF, S)))
+        nc.vector.tensor_copy(xg[1][:], xw[1][:].indirect(offs_t[:]))
         cast(on_vector, 0, 1, 0, 1)
-        cast(on_scalar, 0, 1, 1, 2)
-        cast(on_scalar, 0, 1, 2, 3)
-        cast(on_vector, 0, 1, 3, 4)
+        for t in range(1, TILES):
+            cast(on_scalar, 0, 1, t, t + 1)
         pack(0, 1, 0)
         multiply(0, 1, 0)
+        pack(0, 0, 2, "g0_1_0")
         pack(0, 1, 1)
         multiply(0, 1, 1)
         for t in range(2, TILES):
@@ -176,27 +174,20 @@ def tile_picked_hub_silu_p_kernel(
         fetch_sources(0)
         empty(0, 1)
         fetch_sources(1)
-        cast(on_scalar, 1, 0, 0, 2)
-        cast(on_scalar, 1, 1, 0, 2)
+        cast(on_scalar, 1, 0, 0, 4)
         pack(1, 0, 0)
-        pack(1, 1, 0)
-        for t in range(2):
-            for z in range(PASSES):
-                multiply(1, z, t)
-        empty(0, 2)
+        empty(0, 2, tag="raw1_0")
         fetch_sources(2)
-        cast(on_scalar, 1, 0, 2, 4)
-        pack(1, 0, 2)
-        empty(0, 3)
-        cast(on_scalar, 1, 1, 2, 4)
-        pack(1, 1, 2)
+        cast(on_scalar, 1, 1, 0, 4)
+        pack(1, 1, 0)
+        empty(0, 3, tag="raw1_1")
         fetch_sources(3)
-        for t in range(2, TILES):
+        for t in range(TILES):
             for z in range(PASSES):
                 multiply(1, z, t)
         for t in range(TILES):
             empty(1, t)
-        grouped3 = held([P, N // P, P * PACK], BF16, "g3")
+        grouped3 = held([P, N // P, P * PACK], BF16, "g3", "g1_1_0")
         on_scalar(
             grouped3[:].rearrange("p a (c i j) -> p a c j i", i=RUN, j=PACK),
             raw3[:].rearrange("p j (a c i) -> p a c j i", a=N // P, i=RUN),
@@ -204,12 +195,16 @@ def tile_picked_hub_silu_p_kernel(
 
         sums = {}
         z_in = {}
-        behind = {2: "picked3_0", 3: "z_in0", 4: "z_in1"}
+        behind = {2: "picked3_0", 3: "z_in1", 4: "z_in2"}
 
         def add_targets(u, t):
             lo, hi = SPANS[u]
-            if t == 0:
-                sums[u] = held([P, TILES, hi - lo], F32, "sums%d" % u, behind.get(u))
+            if t == 0 and u < 4:
+                sums[u] = held([P, TILES, hi - lo], F32, "sums%d" % u, behind.get(u))[:]
+            if t == 0 and u == 4:
+                pair = held([P, 2, TILES, hi - lo], F32, "sums%d" % u, behind.get(u))
+                sums[4] = pair[:, 0]
+                sums[5] = pair[:, 1]
             nc.vector.tensor_tensor(
                 sums[u][:, t, :],
                 rows[(1, t)][:].indirect(entries(dst_t, lo, hi)),
@@ -222,7 +217,7 @@ def tile_picked_hub_silu_p_kernel(
             z_in[u] = held([P, (hi - lo) * PACK], BF16, "z_in%d" % u)
             nc.scalar.activation(
                 z_in[u][:].rearrange("p (c i t) -> p c t i", i=RUN, t=TILES),
-                sums[u][:].rearrange("p t (c i) -> p c t i", i=RUN),
+                sums[u].rearrange("p t (c i) -> p c t i", i=RUN),
                 SILU,
             )
 
@@ -257,22 +252,10 @@ def tile_picked_hub_silu_p_kernel(
         words3, scales3 = quantise(grouped3, N // P, "3")
         activate(0)
         activate(1)
-        for t in range(TILES):
-            add_targets(2, t)
-        second_layer(0)
-        activate(2)
-        store(0, on_scalar)
-        for t in range(TILES):
-            add_targets(3, t)
-        second_layer(1)
-        activate(3)
-        store(1, on_scalar)
-        for t in range(TILES):
-            add_targets(4, t)
-        activate(4)
-        second_layer(2)
-        second_layer(3)
-        store(2, on_scalar)
-        second_layer(4)
-        store(3, on_vector)
-        store(4, on_scalar)
+        for u in range(2, len(SPANS)):
+            for t in range(TILES):
+                add_targets(u, t)
+            activate(u)
+            for done in {2: (0, 1), 3: (2,), 5: (3, 4, 5)}.get(u, ()):
+                second_layer(done)
+                store(done, on_scalar)

@@ -100,8 +100,8 @@ def tile_picked_hub_silu_p_kernel(
         woven = {}
         codes = {}
 
-        def cast(copy, which, z, t0, t1):
-            grouped = held([P, t1 - t0, P * PACK], BF16, "g%d_%d_%d" % (which, z, t0))
+        def cast(copy, which, z, t0, t1, tag=None):
+            grouped = held([P, t1 - t0, P * PACK], BF16, "g%d_%d_%d" % (which, z, t0), tag)
             copy(
                 grouped[:].rearrange("p t (c i j) -> p t c j i", i=RUN, j=PACK),
                 raw[(which, z)][:].rearrange("p j (c t i) -> p t c j i", t=TILES, i=RUN)[:, t0:t1],
@@ -142,12 +142,16 @@ def tile_picked_hub_silu_p_kernel(
 
         picked = {}
 
-        def fetch_sources(t, tags=(None, None)):
-            for h in range(2):
-                picked[(t, h)] = held([P, HALF], F32, "picked%d_%d" % (t, h), tags[h])
-                nc.vector.tensor_copy(
-                    picked[(t, h)][:], rows[(0, t)][:].indirect(entries(src_t, h * HALF, (h + 1) * HALF))
-                )
+        def fetch_sources(t, cuts):
+            for lo, hi in cuts:
+                picked[(t, lo)] = held([P, hi - lo], F32, "picked%d_%d" % (t, lo))
+                nc.vector.tensor_copy(picked[(t, lo)][:], rows[(0, t)][:].indirect(entries(src_t, lo, hi)))
+
+        def sources(t, lo, hi):
+            first = max(at for tile, at in picked if tile == t and at <= lo)
+            return picked[(t, first)][:, lo - first : hi - first]
+
+        halves = [(0, HALF), (HALF, S)]
 
         nc.vector.tensor_copy(xg[0][:], xw[0][:].indirect(offs_t[:]))
         nc.vector.tensor_copy(xsg[:], xs[:].indirect(offs_t[:]))
@@ -171,46 +175,34 @@ def tile_picked_hub_silu_p_kernel(
             multiply(0, 0, t)
             multiply(0, 1, t)
         empty(0, 0, (on_scalar, on_vector))
-        fetch_sources(0)
+        fetch_sources(0, halves)
         empty(0, 1)
-        fetch_sources(1)
+        fetch_sources(1, halves)
         cast(on_scalar, 1, 0, 0, 4)
         pack(1, 0, 0)
         empty(0, 2, tag="raw1_0")
-        fetch_sources(2)
+        fetch_sources(2, halves)
         cast(on_scalar, 1, 1, 0, 4)
         pack(1, 1, 0)
         empty(0, 3, tag="raw1_1")
-        fetch_sources(3)
+        fetch_sources(3, SPANS[:2] + halves[1:])
         for t in range(TILES):
             for z in range(PASSES):
                 multiply(1, z, t)
         for t in range(TILES):
             empty(1, t)
         grouped3 = held([P, N // P, P * PACK], BF16, "g3", "g1_1_0")
-        on_scalar(
-            grouped3[:].rearrange("p a (c i j) -> p a c j i", i=RUN, j=PACK),
-            raw3[:].rearrange("p j (a c i) -> p a c j i", a=N // P, i=RUN),
-        )
+        for m in range(N // P):
+            on_scalar(
+                grouped3[:, m, :].rearrange("p (c i j) -> p c j i", i=RUN, j=PACK),
+                raw3[:, :, m * P : (m + 1) * P].rearrange("p j (c i) -> p c j i", i=RUN),
+            )
 
         sums = {}
         z_in = {}
-        behind = {2: "picked3_0", 3: "z_in1", 4: "z_in2"}
 
-        def add_targets(u, t):
-            lo, hi = SPANS[u]
-            if t == 0 and u < 4:
-                sums[u] = held([P, TILES, hi - lo], F32, "sums%d" % u, behind.get(u))[:]
-            if t == 0 and u == 4:
-                pair = held([P, 2, TILES, hi - lo], F32, "sums%d" % u, behind.get(u))
-                sums[4] = pair[:, 0]
-                sums[5] = pair[:, 1]
-            nc.vector.tensor_tensor(
-                sums[u][:, t, :],
-                rows[(1, t)][:].indirect(entries(dst_t, lo, hi)),
-                picked[(t, lo // HALF)][:, lo % HALF : lo % HALF + hi - lo],
-                ADD,
-            )
+        def add_targets(into, t, lo, hi):
+            nc.vector.tensor_tensor(into, rows[(1, t)][:].indirect(entries(dst_t, lo, hi)), sources(t, lo, hi), ADD)
 
         def activate(u):
             lo, hi = SPANS[u]
@@ -246,15 +238,24 @@ def tile_picked_hub_silu_p_kernel(
             copy(result[:], outs[u][:])
             nc.sync.dma_start(out=out[:, lo:hi].rearrange("(m p) r -> p m r", p=P), in_=result[:])
 
-        for t in range(TILES):
-            for u in range(2):
-                add_targets(u, t)
+        front = held([P, TILES, HALF], F32, "front")
+        for t in range(TILES - 1):
+            add_targets(front[:, t, :], t, 0, HALF)
+        for u in range(2):
+            lo, hi = SPANS[u]
+            sums[u] = front[:, :, lo:hi]
+            add_targets(sums[u][:, TILES - 1, :], TILES - 1, lo, hi)
         words3, scales3 = quantise(grouped3, N // P, "3")
         activate(0)
         activate(1)
+        sums[2] = held([P, TILES, 256], F32, "sums2", "picked3_0")[:]
+        sums[3] = held([P, TILES, 128], F32, "sums3", "front")[:]
+        pair = held([P, 2, TILES, 64], F32, "sums4", "picked3_0")
+        sums[4] = pair[:, 0]
+        sums[5] = pair[:, 1]
         for u in range(2, len(SPANS)):
             for t in range(TILES):
-                add_targets(u, t)
+                add_targets(sums[u][:, t, :], t, *SPANS[u])
             activate(u)
             for done in {2: (0, 1), 3: (2,), 5: (3, 4, 5)}.get(u, ()):
                 second_layer(done)

@@ -61,17 +61,17 @@ def tile_picked_hub_silu_p_kernel(
             nc.sync.dma_start(out=raw[(which, z)][:], in_=rows.rearrange("(p j) c -> p j c", j=PACK))
 
         nc.vector.memset(xs[:].bitcast(I32), 0)
-        load_words(0)
         nc.sync.dma_start(offs_t[:], offs)
+        nc.sync.dma_start(src_t[:], src)
         for q in range(4):
             nc.sync.dma_start(
                 out=xs[32 * q : 32 * q + 4 * PASSES, :].bitcast(I32),
                 in_=x_scales[:, 4 * q : 4 * q + 4, :].bitcast(I32),
             )
+        load_words(0)
         load_pass(0, w1, 0)
         load_words(1)
         load_pass(0, w1, 1)
-        nc.sync.dma_start(src_t[:], src)
         load_pass(1, w2, 0)
         nc.sync.dma_start(dst_t[:], dst)
         load_pass(1, w2, 1)
@@ -153,26 +153,25 @@ def tile_picked_hub_silu_p_kernel(
 
         halves = [(0, HALF), (HALF, S)]
 
-        nc.vector.tensor_copy(xg[0][:], xw[0][:].indirect(offs_t[:]))
         nc.vector.tensor_copy(xsg[:], xs[:].indirect(offs_t[:]))
+        nc.vector.tensor_copy(xg[0][:], xw[0][:].indirect(offs_t[:]))
         cast(on_scalar, 0, 0, 0, 2)
-        cast(on_scalar, 0, 0, 2, 4)
+        cast(on_vector, 0, 0, 2, 4)
         pack(0, 0, 0)
-        multiply(0, 0, 0)
-        multiply(0, 0, 1)
-        xg.append(held([P, S], U32, "xg1", "xs"))
+        pack(0, 0, 2)
+        for t in range(TILES):
+            multiply(0, 0, t)
+        xg.append(held([P, S], U32, "xg1"))
         nc.vector.tensor_copy(xg[1][:], xw[1][:].indirect(offs_t[:]))
         cast(on_vector, 0, 1, 0, 1)
-        for t in range(1, TILES):
-            cast(on_scalar, 0, 1, t, t + 1)
         pack(0, 1, 0)
         multiply(0, 1, 0)
-        pack(0, 0, 2, "g0_1_0")
+        cast(on_scalar, 0, 1, 1, 2)
         pack(0, 1, 1)
         multiply(0, 1, 1)
         for t in range(2, TILES):
+            cast(on_vector, 0, 1, t, t + 1, "g0_1_0" if t == 2 else "g0_1_1")
             pack(0, 1, t)
-            multiply(0, 0, t)
             multiply(0, 1, t)
         empty(0, 0, (on_scalar, on_vector))
         fetch_sources(0, halves)

@@ -47,10 +47,10 @@ def tile_picked_hub_silu_p_kernel(
         xw = [held([P, T], U32, "xw%d" % z) for z in range(PASSES)]
         xs = held([P, T], U8, "xs")
 
-        def load_words(z):
+        def load_words(z, lo=0, hi=T):
             nc.sync.dma_start(
-                out=xw[z][:].bitcast(I32),
-                in_=x_words[z].rearrange("p n t -> p (n t)").bitcast(I32),
+                out=xw[z][:, lo:hi].bitcast(I32),
+                in_=x_words[z].rearrange("p n t -> p (n t)").bitcast(I32)[:, lo:hi],
             )
 
         raw = {}
@@ -62,16 +62,17 @@ def tile_picked_hub_silu_p_kernel(
 
         nc.vector.memset(xs[:].bitcast(I32), 0)
         nc.sync.dma_start(offs_t[:], offs)
-        nc.sync.dma_start(src_t[:], src)
+        load_words(0, 0, T // 4)
         for q in range(4):
             nc.sync.dma_start(
                 out=xs[32 * q : 32 * q + 4 * PASSES, :].bitcast(I32),
                 in_=x_scales[:, 4 * q : 4 * q + 4, :].bitcast(I32),
             )
-        load_words(0)
+        load_words(0, T // 4, T)
         load_pass(0, w1, 0)
         load_words(1)
         load_pass(0, w1, 1)
+        nc.sync.dma_start(src_t[:], src)
         load_pass(1, w2, 0)
         nc.sync.dma_start(dst_t[:], dst)
         load_pass(1, w2, 1)
@@ -123,7 +124,7 @@ def tile_picked_hub_silu_p_kernel(
             words, scales = codes[(which, z, t)]
             for h in range(2):
                 if z == 0:
-                    acc[(which, t, h)] = bank(2 * t + h, [P, HALF], "acc%d_%d_%d" % (which, t, h))
+                    acc[(which, t, h)] = bank(2 * (t if which else t % 2) + h, [P, HALF], "acc%d_%d_%d" % (which, t, h))
                 cols = slice(h * HALF, (h + 1) * HALF)
                 nc.tensor.matmul_mx(
                     out=acc[(which, t, h)][:],
@@ -136,7 +137,7 @@ def tile_picked_hub_silu_p_kernel(
                 )
 
         def empty(which, t, copies=(on_scalar, on_scalar), tag=None):
-            rows[(which, t)] = held([P, S], F32, "row%d_%d" % (which, t), tag)
+            rows[(which, t)] = held([P, (2 - which) * S], F32, "row%d_%d" % (which, t), tag)
             for h in range(2):
                 copies[h](rows[(which, t)][:, h * HALF : (h + 1) * HALF], acc[(which, t, h)][:])
 
@@ -156,10 +157,12 @@ def tile_picked_hub_silu_p_kernel(
         nc.vector.tensor_copy(xsg[:], xs[:].indirect(offs_t[:]))
         nc.vector.tensor_copy(xg[0][:], xw[0][:].indirect(offs_t[:]))
         cast(on_scalar, 0, 0, 0, 2)
-        cast(on_vector, 0, 0, 2, 4)
+        cast(on_scalar, 0, 0, 2, 3)
+        cast(on_vector, 0, 0, 3, 4)
         pack(0, 0, 0)
         pack(0, 0, 2)
-        for t in range(TILES):
+        pack(0, 0, 3)
+        for t in range(2):
             multiply(0, 0, t)
         xg.append(held([P, S], U32, "xg1"))
         nc.vector.tensor_copy(xg[1][:], xw[1][:].indirect(offs_t[:]))
@@ -172,19 +175,22 @@ def tile_picked_hub_silu_p_kernel(
         for t in range(2, TILES):
             cast(on_vector, 0, 1, t, t + 1, "g0_1_0" if t == 2 else "g0_1_1")
             pack(0, 1, t)
-            multiply(0, 1, t)
-        empty(0, 0, (on_scalar, on_vector))
-        fetch_sources(0, halves)
-        empty(0, 1)
-        fetch_sources(1, halves)
+        empty(0, 0, (on_scalar, on_vector), "raw0_0")
+        multiply(0, 0, 2)
+        multiply(0, 1, 2)
+        fetch_sources(0, [(0, S)])
+        empty(0, 1, tag="xw0")
+        multiply(0, 0, 3)
+        multiply(0, 1, 3)
+        fetch_sources(1, [(0, S)])
         cast(on_scalar, 1, 0, 0, 4)
         pack(1, 0, 0)
         empty(0, 2, tag="raw1_0")
-        fetch_sources(2, halves)
+        fetch_sources(2, [(0, S)])
         cast(on_scalar, 1, 1, 0, 4)
         pack(1, 1, 0)
         empty(0, 3, tag="raw1_1")
-        fetch_sources(3, SPANS[:2] + halves[1:])
+        fetch_sources(3, [(0, 256), (256, S)])
         for t in range(TILES):
             for z in range(PASSES):
                 multiply(1, z, t)

@@ -74,8 +74,8 @@ def tile_picked_hub_silu_p_kernel(
         load_pass(0, w1, 1)
         nc.sync.dma_start(src_t[:], src)
         load_pass(1, w2, 0)
-        nc.sync.dma_start(dst_t[:], dst)
         load_pass(1, w2, 1)
+        nc.sync.dma_start(dst_t[:], dst)
         raw3 = held([P, TILES, N], F32, "raw3")
         w3_rows = w3.rearrange("(c t i) m -> t c i m", t=TILES, i=RUN)
         for t in range(TILES):
@@ -183,20 +183,22 @@ def tile_picked_hub_silu_p_kernel(
         multiply(0, 0, 3)
         multiply(0, 1, 3)
         fetch_sources(1, [(0, S)])
-        cast(on_scalar, 1, 0, 0, 4)
+        cast(on_scalar, 1, 0, 0, 4, "xw1")
         pack(1, 0, 0)
         empty(0, 2, tag="raw1_0")
         fetch_sources(2, [(0, S)])
-        cast(on_scalar, 1, 1, 0, 4)
+        cast(on_scalar, 1, 1, 0, 2)
         pack(1, 1, 0)
-        empty(0, 3, tag="raw1_1")
+        empty(0, 3, tag="xw1")
+        cast(on_scalar, 1, 1, 2, 4)
+        pack(1, 1, 2)
         fetch_sources(3, [(0, 256), (256, S)])
         for t in range(TILES):
             for z in range(PASSES):
                 multiply(1, z, t)
         for t in range(TILES):
             empty(1, t)
-        grouped3 = held([P, N // P, P * PACK], BF16, "g3", "g1_1_0")
+        grouped3 = held([P, N // P, P * PACK], BF16, "g3", "g1_1_2")
         for m in range(N // P):
             on_scalar(
                 grouped3[:, m, :].rearrange("p (c i j) -> p c j i", i=RUN, j=PACK),
@@ -255,11 +257,14 @@ def tile_picked_hub_silu_p_kernel(
         activate(1)
         sums[2] = held([P, TILES, 256], F32, "sums2", "picked3_0")[:]
         sums[3] = held([P, TILES, 128], F32, "sums3", "front")[:]
-        pair = held([P, 2, TILES, 64], F32, "sums4", "picked3_0")
-        sums[4] = pair[:, 0]
-        sums[5] = pair[:, 1]
+        pair = held([P, TILES, 128], F32, "sums4", "picked3_0")
+        sums[4] = pair[:, :, 0:64]
+        sums[5] = pair[:, :, 64:128]
         for u in range(2, len(SPANS)):
-            for t in range(TILES):
+            if u == 4:
+                for t in range(TILES - 1):
+                    add_targets(pair[:, t, :], t, SPANS[4][0], S)
+            for t in range(TILES) if u < 4 else [TILES - 1]:
                 add_targets(sums[u][:, t, :], t, *SPANS[u])
             activate(u)
             for done in {2: (0, 1), 3: (2,), 5: (3, 4, 5)}.get(u, ()):

@@ -14,6 +14,7 @@ U8 = mybir.dt.uint8
 FP8X4 = mybir.dt.float8_e4m3fn_x4
 SILU = mybir.ActivationFunctionType.Silu
 ADD = mybir.AluOpType.add
+MULT = mybir.AluOpType.mult
 
 P = 128
 PACK = 4
@@ -30,9 +31,12 @@ def tile_picked_hub_silu_p_kernel(
     nc = tc.nc
     with ExitStack() as ctx:
         keep = ctx.enter_context(tc.tile_pool(name="keep", bufs=1))
+        laid = ctx.enter_context(tc.tile_pool(name="laid", bufs=1))
         psum = ctx.enter_context(tc.psum_pool(name="psum", bufs=1))
 
         def held(shape, dtype, name, tag=None):
+            if isinstance(tag, int):
+                return laid.tile(shape, dtype, name=name, tag=name, align_bytes=64, offset=tag)
             return keep.tile(shape, dtype, name=name, tag=tag or name, align_bytes=64)
 
         def bank(b, shape, name):
@@ -44,7 +48,7 @@ def tile_picked_hub_silu_p_kernel(
         offs_t = held([P, S // 16], U16, "offs_t")
         src_t = held([P, S // 16], U16, "src_t")
         dst_t = held([P, S // 16], U16, "dst_t")
-        xw = [held([P, T], U32, "xw%d" % z) for z in range(PASSES)]
+        xw = [held([P, T], U32, "xw0"), held([P, T], U32, "xw1", 0)]
         xs = held([P, T], U8, "xs")
 
         def load_words(z, lo=0, hi=T):
@@ -143,9 +147,9 @@ def tile_picked_hub_silu_p_kernel(
 
         picked = {}
 
-        def fetch_sources(t, cuts):
+        def fetch_sources(t, cuts, tag=None):
             for lo, hi in cuts:
-                picked[(t, lo)] = held([P, hi - lo], F32, "picked%d_%d" % (t, lo))
+                picked[(t, lo)] = held([P, hi - lo], F32, "picked%d_%d" % (t, lo), tag)
                 nc.vector.tensor_copy(picked[(t, lo)][:], rows[(0, t)][:].indirect(entries(src_t, lo, hi)))
 
         def sources(t, lo, hi):
@@ -183,26 +187,31 @@ def tile_picked_hub_silu_p_kernel(
         multiply(0, 0, 3)
         multiply(0, 1, 3)
         fetch_sources(1, [(0, S)])
-        cast(on_scalar, 1, 0, 0, 4, "xw1")
+        cast(on_scalar, 1, 0, 0, 4, 6144)
         pack(1, 0, 0)
         empty(0, 2, tag="raw1_0")
         fetch_sources(2, [(0, S)])
-        cast(on_scalar, 1, 1, 0, 2)
+        cast(on_scalar, 1, 1, 0, 2, 10240)
         pack(1, 1, 0)
-        empty(0, 3, tag="xw1")
+        empty(0, 3, tag=0)
         cast(on_scalar, 1, 1, 2, 4)
         pack(1, 1, 2)
-        fetch_sources(3, [(0, 256), (256, S)])
+        fetch_sources(3, [(0, 256)], 16384 + 512)
+        fetch_sources(3, [(256, S)])
         for t in range(TILES):
             for z in range(PASSES):
                 multiply(1, z, t)
         for t in range(TILES):
             empty(1, t)
-        grouped3 = held([P, N // P, P * PACK], BF16, "g3", "g1_1_2")
+        grouped3 = [held([P, 1, P * PACK], BF16, "g3_%d" % m, 8192 + 2048 * m) for m in range(N // P)]
         for m in range(N // P):
-            on_scalar(
-                grouped3[:, m, :].rearrange("p (c i j) -> p c j i", i=RUN, j=PACK),
-                raw3[:, :, m * P : (m + 1) * P].rearrange("p j (c i) -> p c j i", i=RUN),
+            nc.gpsimd.tensor_scalar(
+                grouped3[m][:, 0, :].rearrange("p (c j) -> p c j", j=PACK),
+                raw3[:, :, m * P : (m + 1) * P].rearrange("p j c -> p c j"),
+                1.0,
+                0.0,
+                MULT,
+                ADD,
             )
 
         sums = {}
@@ -231,8 +240,8 @@ def tile_picked_hub_silu_p_kernel(
             for m in range(N // P):
                 nc.tensor.matmul_mx(
                     out=outs[u][:, m, :],
-                    lhsT=words3[:, m, :].bitcast(FP8X4),
-                    lhsT_scale=scales3[:, m, :],
+                    lhsT=codes3[m][0][:, 0, :].bitcast(FP8X4),
+                    lhsT_scale=codes3[m][1][:, 0, :],
                     rhs=words[:].bitcast(FP8X4),
                     rhs_scale=scales[:],
                     start=True,
@@ -252,12 +261,12 @@ def tile_picked_hub_silu_p_kernel(
             lo, hi = SPANS[u]
             sums[u] = front[:, :, lo:hi]
             add_targets(sums[u][:, TILES - 1, :], TILES - 1, lo, hi)
-        words3, scales3 = quantise(grouped3, N // P, "3")
+        codes3 = [quantise(grouped3[m], 1, "3_%d" % m, 16384 + 64 + 512 * m) for m in range(N // P)]
         activate(0)
         activate(1)
-        sums[2] = held([P, TILES, 256], F32, "sums2", "picked3_0")[:]
+        sums[2] = held([P, TILES, 256], F32, "sums2", 16384 + 1088)[:]
         sums[3] = held([P, TILES, 128], F32, "sums3", "front")[:]
-        pair = held([P, TILES, 128], F32, "sums4", "picked3_0")
+        pair = held([P, TILES, 128], F32, "sums4", 16384 + 1088)
         sums[4] = pair[:, :, 0:64]
         sums[5] = pair[:, :, 64:128]
         for u in range(2, len(SPANS)):

@@ -12,6 +12,7 @@ U32 = mybir.dt.uint32
 U16 = mybir.dt.uint16
 U8 = mybir.dt.uint8
 FP8X4 = mybir.dt.float8_e4m3fn_x4
+COPY = mybir.ActivationFunctionType.Copy
 SILU = mybir.ActivationFunctionType.Silu
 ADD = mybir.AluOpType.add
 MULT = mybir.AluOpType.mult
@@ -22,6 +23,7 @@ PASSES = K // (P * PACK)
 HALF = 512
 TILES = H // P
 RUN = 4
+SPARE = 16
 SPANS = [(0, 256), (256, 512), (512, 768), (768, 896), (896, 960), (960, 1024)]
 
 
@@ -48,7 +50,7 @@ def tile_picked_hub_silu_p_kernel(
         offs_t = held([P, S // 16], U16, "offs_t")
         src_t = held([P, S // 16], U16, "src_t")
         dst_t = held([P, S // 16], U16, "dst_t")
-        xw = [held([P, T], U32, "xw0"), held([P, T], U32, "xw1", 0)]
+        xw = [held([P, T], U32, "xw0"), held([P, T], U32, "xw1")]
         xs = held([P, T], U8, "xs")
 
         def load_words(z, lo=0, hi=T):
@@ -128,7 +130,7 @@ def tile_picked_hub_silu_p_kernel(
             words, scales = codes[(which, z, t)]
             for h in range(2):
                 if z == 0:
-                    acc[(which, t, h)] = bank(2 * (t if which else t % 2) + h, [P, HALF], "acc%d_%d_%d" % (which, t, h))
+                    acc[(which, t, h)] = bank(4 * which + 2 * (t % 2) + h, [P, HALF], "acc%d_%d_%d" % (which, t, h))
                 cols = slice(h * HALF, (h + 1) * HALF)
                 nc.tensor.matmul_mx(
                     out=acc[(which, t, h)][:],
@@ -140,8 +142,8 @@ def tile_picked_hub_silu_p_kernel(
                     stop=(z == PASSES - 1),
                 )
 
-        def empty(which, t, copies=(on_scalar, on_scalar), tag=None):
-            rows[(which, t)] = held([P, (2 - which) * S], F32, "row%d_%d" % (which, t), tag)
+        def empty(which, t, copies, tag=None):
+            rows[(which, t)] = held([P, S + (0 if which else SPARE)], F32, "row%d_%d" % (which, t), tag)
             for h in range(2):
                 copies[h](rows[(which, t)][:, h * HALF : (h + 1) * HALF], acc[(which, t, h)][:])
 
@@ -150,13 +152,11 @@ def tile_picked_hub_silu_p_kernel(
         def fetch_sources(t, cuts, tag=None):
             for lo, hi in cuts:
                 picked[(t, lo)] = held([P, hi - lo], F32, "picked%d_%d" % (t, lo), tag)
-                nc.vector.tensor_copy(picked[(t, lo)][:], rows[(0, t)][:].indirect(entries(src_t, lo, hi)))
+                nc.scalar.activation(picked[(t, lo)][:], rows[(0, t)][:].indirect(entries(src_t, lo, hi)), COPY)
 
         def sources(t, lo, hi):
             first = max(at for tile, at in picked if tile == t and at <= lo)
             return picked[(t, first)][:, lo - first : hi - first]
-
-        halves = [(0, HALF), (HALF, S)]
 
         nc.vector.tensor_copy(xsg[:], xs[:].indirect(offs_t[:]))
         nc.vector.tensor_copy(xg[0][:], xw[0][:].indirect(offs_t[:]))
@@ -183,27 +183,29 @@ def tile_picked_hub_silu_p_kernel(
         multiply(0, 0, 2)
         multiply(0, 1, 2)
         fetch_sources(0, [(0, S)])
-        empty(0, 1, tag="xw0")
+        empty(0, 1, (on_scalar, on_scalar), "xw0")
         multiply(0, 0, 3)
         multiply(0, 1, 3)
         fetch_sources(1, [(0, S)])
-        cast(on_scalar, 1, 0, 0, 4, 6144)
-        pack(1, 0, 0)
-        empty(0, 2, tag="raw1_0")
+        empty(0, 2, (on_scalar, on_scalar), "raw0_1")
         fetch_sources(2, [(0, S)])
-        cast(on_scalar, 1, 1, 0, 2, 10240)
+        empty(0, 3, (on_scalar, on_scalar), "xw1")
+        fetch_sources(3, [(0, HALF)], 16384)
+        fetch_sources(3, [(HALF, S)])
+
+        cast(on_vector, 1, 0, 0, 2)
+        cast(on_vector, 1, 0, 2, 4)
+        pack(1, 0, 0)
+        pack(1, 0, 2)
+        cast(on_vector, 1, 1, 0, 2)
+        cast(on_vector, 1, 1, 2, 4, 0)
         pack(1, 1, 0)
-        empty(0, 3, tag=0)
-        cast(on_scalar, 1, 1, 2, 4)
-        pack(1, 1, 2)
-        fetch_sources(3, [(0, 256)], 16384 + 512)
-        fetch_sources(3, [(256, S)])
+        pack(1, 1, 2, 8192 + 4096)
         for t in range(TILES):
             for z in range(PASSES):
                 multiply(1, z, t)
-        for t in range(TILES):
-            empty(1, t)
-        grouped3 = [held([P, 1, P * PACK], BF16, "g3_%d" % m, 8192 + 2048 * m) for m in range(N // P)]
+            empty(1, t, (on_vector, on_vector))
+        grouped3 = [held([P, 1, P * PACK], BF16, "g3_%d" % m, 1024 * m) for m in range(N // P)]
         for m in range(N // P):
             nc.gpsimd.tensor_scalar(
                 grouped3[m][:, 0, :].rearrange("p (c j) -> p c j", j=PACK),
@@ -254,19 +256,19 @@ def tile_picked_hub_silu_p_kernel(
             copy(result[:], outs[u][:])
             nc.sync.dma_start(out=out[:, lo:hi].rearrange("(m p) r -> p m r", p=P), in_=result[:])
 
-        front = held([P, TILES, HALF], F32, "front")
+        front = held([P, TILES, HALF], F32, "front", 4096 + 1024)
         for t in range(TILES - 1):
             add_targets(front[:, t, :], t, 0, HALF)
         for u in range(2):
             lo, hi = SPANS[u]
             sums[u] = front[:, :, lo:hi]
             add_targets(sums[u][:, TILES - 1, :], TILES - 1, lo, hi)
-        codes3 = [quantise(grouped3[m], 1, "3_%d" % m, 16384 + 64 + 512 * m) for m in range(N // P)]
+        codes3 = [quantise(grouped3[m], 1, "3_%d" % m, 16384 + 512 * m) for m in range(N // P)]
         activate(0)
         activate(1)
-        sums[2] = held([P, TILES, 256], F32, "sums2", 16384 + 1088)[:]
-        sums[3] = held([P, TILES, 128], F32, "sums3", "front")[:]
-        pair = held([P, TILES, 128], F32, "sums4", 16384 + 1088)
+        sums[2] = held([P, TILES, 256], F32, "sums2", 16384 + 1024)[:]
+        sums[3] = held([P, TILES, 128], F32, "sums3", 4096 + 1024)[:]
+        pair = held([P, TILES, 128], F32, "sums4", 16384 + 1024)
         sums[4] = pair[:, :, 0:64]
         sums[5] = pair[:, :, 64:128]
         for u in range(2, len(SPANS)):

@@ -149,14 +149,14 @@ def tile_picked_hub_silu_p_kernel(
 
         picked = {}
 
-        def fetch_sources(t, cuts, tag=None):
-            for lo, hi in cuts:
-                picked[(t, lo)] = held([P, hi - lo], F32, "picked%d_%d" % (t, lo), tag)
-                nc.scalar.activation(picked[(t, lo)][:], rows[(0, t)][:].indirect(entries(src_t, lo, hi)), COPY)
+        def fetch_sources(t, h, into=None):
+            if into is None:
+                into = held([P, HALF], F32, "picked%d_%d" % (t, h))[:]
+            picked[(t, h)] = into
+            nc.scalar.activation(into, rows[(0, t)][:].indirect(entries(src_t, h * HALF, (h + 1) * HALF)), COPY)
 
         def sources(t, lo, hi):
-            first = max(at for tile, at in picked if tile == t and at <= lo)
-            return picked[(t, first)][:, lo - first : hi - first]
+            return picked[(t, lo // HALF)][:, lo % HALF : lo % HALF + hi - lo]
 
         nc.vector.tensor_copy(xsg[:], xs[:].indirect(offs_t[:]))
         nc.vector.tensor_copy(xg[0][:], xw[0][:].indirect(offs_t[:]))
@@ -182,16 +182,17 @@ def tile_picked_hub_silu_p_kernel(
         empty(0, 0, (on_scalar, on_vector), "raw0_0")
         multiply(0, 0, 2)
         multiply(0, 1, 2)
-        fetch_sources(0, [(0, S)])
+        fetch_sources(0, 0)
         empty(0, 1, (on_scalar, on_scalar), "xw0")
         multiply(0, 0, 3)
         multiply(0, 1, 3)
-        fetch_sources(1, [(0, S)])
+        fetch_sources(0, 1)
+        fetch_sources(1, 0)
         empty(0, 2, (on_scalar, on_scalar), "raw0_1")
-        fetch_sources(2, [(0, S)])
+        fetch_sources(1, 1)
+        fetch_sources(2, 0)
         empty(0, 3, (on_scalar, on_scalar), "xw1")
-        fetch_sources(3, [(0, HALF)], 16384)
-        fetch_sources(3, [(HALF, S)])
+        fetch_sources(3, 0, held([P, HALF], F32, "picked3_0", 18432)[:])
 
         cast(on_vector, 1, 0, 0, 2)
         cast(on_vector, 1, 0, 2, 4)
@@ -200,11 +201,14 @@ def tile_picked_hub_silu_p_kernel(
         cast(on_vector, 1, 1, 0, 2)
         cast(on_vector, 1, 1, 2, 4, 0)
         pack(1, 1, 0)
-        pack(1, 1, 2, 8192 + 4096)
+        pack(1, 1, 2, 12288)
         for t in range(TILES):
             for z in range(PASSES):
                 multiply(1, z, t)
-            empty(1, t, (on_vector, on_vector))
+            empty(1, t, (on_vector, on_vector) if t < TILES - 1 else (on_scalar, on_scalar))
+        late = held([P, 2, HALF], F32, "late", 13312 - 64)
+        for t in range(2, TILES):
+            fetch_sources(t, 1, late[:, t - 2, :])
         grouped3 = [held([P, 1, P * PACK], BF16, "g3_%d" % m, 1024 * m) for m in range(N // P)]
         for m in range(N // P):
             nc.gpsimd.tensor_scalar(
@@ -256,19 +260,19 @@ def tile_picked_hub_silu_p_kernel(
             copy(result[:], outs[u][:])
             nc.sync.dma_start(out=out[:, lo:hi].rearrange("(m p) r -> p m r", p=P), in_=result[:])
 
-        front = held([P, TILES, HALF], F32, "front", 4096 + 1024)
+        front = held([P, TILES, HALF], F32, "front", 4096 + 64)
         for t in range(TILES - 1):
             add_targets(front[:, t, :], t, 0, HALF)
         for u in range(2):
             lo, hi = SPANS[u]
             sums[u] = front[:, :, lo:hi]
             add_targets(sums[u][:, TILES - 1, :], TILES - 1, lo, hi)
-        codes3 = [quantise(grouped3[m], 1, "3_%d" % m, 16384 + 512 * m) for m in range(N // P)]
+        codes3 = [quantise(grouped3[m], 1, "3_%d" % m, 18432 + 512 * m) for m in range(N // P)]
         activate(0)
         activate(1)
-        sums[2] = held([P, TILES, 256], F32, "sums2", 16384 + 1024)[:]
-        sums[3] = held([P, TILES, 128], F32, "sums3", 4096 + 1024)[:]
-        pair = held([P, TILES, 128], F32, "sums4", 16384 + 1024)
+        sums[2] = held([P, TILES, 256], F32, "sums2", 18432 + 1024)[:]
+        sums[3] = held([P, TILES, 128], F32, "sums3", 4096 + 64)[:]
+        pair = held([P, TILES, 128], F32, "sums4", 18432 + 1024)
         sums[4] = pair[:, :, 0:64]
         sums[5] = pair[:, :, 64:128]
         for u in range(2, len(SPANS)):

@@ -23,7 +23,6 @@ PASSES = K // (P * PACK)
 HALF = 512
 TILES = H // P
 RUN = 4
-SPARE = 16
 SPANS = [(0, 256), (256, 512), (512, 768), (768, 896), (896, 960), (960, 1024)]
 
 
@@ -82,7 +81,7 @@ def tile_picked_hub_silu_p_kernel(
         load_pass(1, w2, 0)
         load_pass(1, w2, 1)
         nc.sync.dma_start(dst_t[:], dst)
-        raw3 = held([P, TILES, N], F32, "raw3")
+        raw3 = held([P, TILES, N], F32, "raw3", 4096)
         w3_rows = w3.rearrange("(c t i) m -> t c i m", t=TILES, i=RUN)
         for t in range(TILES):
             nc.sync.dma_start(out=raw3[:, t, :], in_=w3_rows[t])
@@ -126,9 +125,9 @@ def tile_picked_hub_silu_p_kernel(
         acc = {}
         rows = {}
 
-        def multiply(which, z, t):
+        def multiply(which, z, t, halves=(0, 1)):
             words, scales = codes[(which, z, t)]
-            for h in range(2):
+            for h in halves:
                 if z == 0:
                     acc[(which, t, h)] = bank(4 * which + 2 * (t % 2) + h, [P, HALF], "acc%d_%d_%d" % (which, t, h))
                 cols = slice(h * HALF, (h + 1) * HALF)
@@ -142,10 +141,10 @@ def tile_picked_hub_silu_p_kernel(
                     stop=(z == PASSES - 1),
                 )
 
-        def empty(which, t, copies, tag=None):
-            rows[(which, t)] = held([P, S + (0 if which else SPARE)], F32, "row%d_%d" % (which, t), tag)
-            for h in range(2):
-                copies[h](rows[(which, t)][:, h * HALF : (h + 1) * HALF], acc[(which, t, h)][:])
+        def empty(copy, which, t, h):
+            if h == 0:
+                rows[(which, t)] = held([P, S], F32, "row%d_%d" % (which, t))
+            copy(rows[(which, t)][:, h * HALF : (h + 1) * HALF], acc[(which, t, h)][:])
 
         picked = {}
 
@@ -176,43 +175,42 @@ def tile_picked_hub_silu_p_kernel(
         cast(on_scalar, 0, 1, 1, 2)
         pack(0, 1, 1)
         multiply(0, 1, 1)
-        for t in range(2, TILES):
-            cast(on_vector, 0, 1, t, t + 1, "g0_1_0" if t == 2 else "g0_1_1")
-            pack(0, 1, t)
-        empty(0, 0, (on_scalar, on_vector), "raw0_0")
-        multiply(0, 0, 2)
-        multiply(0, 1, 2)
-        fetch_sources(0, 0)
-        empty(0, 1, (on_scalar, on_scalar), "xw0")
-        multiply(0, 0, 3)
-        multiply(0, 1, 3)
-        fetch_sources(0, 1)
-        fetch_sources(1, 0)
-        empty(0, 2, (on_scalar, on_scalar), "raw0_1")
-        fetch_sources(1, 1)
-        fetch_sources(2, 0)
-        empty(0, 3, (on_scalar, on_scalar), "xw1")
-        fetch_sources(3, 0, held([P, HALF], F32, "picked3_0", 18432)[:])
+        cast(on_scalar, 0, 1, 2, 4)
+        empty(on_vector, 0, 0, 0)
+        pack(0, 1, 2)
+        empty(on_scalar, 0, 0, 1)
+        for t in range(1, TILES):
+            for h in range(2):
+                if t > 1:
+                    for z in range(PASSES):
+                        multiply(0, z, t, (h,))
+                empty(on_scalar, 0, t, h)
+            fetch_sources(t - 1, 0, held([P, HALF], F32, "picked%d_0" % (t - 1), "c0_1_1" if t == 1 else None)[:])
+        fetch_sources(3, 0, held([P, HALF], F32, "picked3_0", 24576)[:])
 
         cast(on_vector, 1, 0, 0, 2)
         cast(on_vector, 1, 0, 2, 4)
         pack(1, 0, 0)
         pack(1, 0, 2)
-        cast(on_vector, 1, 1, 0, 2)
-        cast(on_vector, 1, 1, 2, 4, 0)
+        cast(on_vector, 1, 1, 0, 1)
+        cast(on_vector, 1, 1, 1, 2)
         pack(1, 1, 0)
+        cast(on_vector, 1, 1, 2, 4, 0)
+        pack(1, 1, 1)
         pack(1, 1, 2, 12288)
         for t in range(TILES):
-            for z in range(PASSES):
-                multiply(1, z, t)
-            empty(1, t, (on_vector, on_vector) if t < TILES - 1 else (on_scalar, on_scalar))
-        late = held([P, 2, HALF], F32, "late", 13312 - 64)
-        for t in range(2, TILES):
-            fetch_sources(t, 1, late[:, t - 2, :])
-        grouped3 = [held([P, 1, P * PACK], BF16, "g3_%d" % m, 1024 * m) for m in range(N // P)]
+            for h in range(2):
+                for z in range(PASSES):
+                    multiply(1, z, t, (h,))
+            empty(on_vector, 1, t, 0)
+            empty(on_vector if t < TILES - 1 else on_scalar, 1, t, 1)
+        late = held([P, TILES, HALF], F32, "late", 13312 - 64)
+        for t in range(TILES):
+            fetch_sources(t, 1, late[:, t, :])
+        grouped3 = held([P, N // P, P * PACK], BF16, "g3", 0)
         for m in range(N // P):
             nc.gpsimd.tensor_scalar(
-                grouped3[m][:, 0, :].rearrange("p (c j) -> p c j", j=PACK),
+                grouped3[:, m, :].rearrange("p (c j) -> p c j", j=PACK),
                 raw3[:, :, m * P : (m + 1) * P].rearrange("p j c -> p c j"),
                 1.0,
                 0.0,
@@ -246,8 +244,8 @@ def tile_picked_hub_silu_p_kernel(
             for m in range(N // P):
                 nc.tensor.matmul_mx(
                     out=outs[u][:, m, :],
-                    lhsT=codes3[m][0][:, 0, :].bitcast(FP8X4),
-                    lhsT_scale=codes3[m][1][:, 0, :],
+                    lhsT=codes3[0][:, m, :].bitcast(FP8X4),
+                    lhsT_scale=codes3[1][:, m, :],
                     rhs=words[:].bitcast(FP8X4),
                     rhs_scale=scales[:],
                     start=True,
@@ -260,19 +258,19 @@ def tile_picked_hub_silu_p_kernel(
             copy(result[:], outs[u][:])
             nc.sync.dma_start(out=out[:, lo:hi].rearrange("(m p) r -> p m r", p=P), in_=result[:])
 
-        front = held([P, TILES, HALF], F32, "front", 4096 + 64)
+        front = held([P, TILES, HALF], F32, "front", 4096)
         for t in range(TILES - 1):
             add_targets(front[:, t, :], t, 0, HALF)
         for u in range(2):
             lo, hi = SPANS[u]
             sums[u] = front[:, :, lo:hi]
             add_targets(sums[u][:, TILES - 1, :], TILES - 1, lo, hi)
-        codes3 = [quantise(grouped3[m], 1, "3_%d" % m, 18432 + 512 * m) for m in range(N // P)]
+        codes3 = quantise(grouped3, N // P, "3", 24576)
         activate(0)
         activate(1)
-        sums[2] = held([P, TILES, 256], F32, "sums2", 18432 + 1024)[:]
-        sums[3] = held([P, TILES, 128], F32, "sums3", 4096 + 64)[:]
-        pair = held([P, TILES, 128], F32, "sums4", 18432 + 1024)
+        sums[2] = held([P, TILES, 256], F32, "sums2", 24576 + 1024)[:]
+        sums[3] = held([P, TILES, 128], F32, "sums3", 4096)[:]
+        pair = held([P, TILES, 128], F32, "sums4", 24576 + 1024)
         sums[4] = pair[:, :, 0:64]
         sums[5] = pair[:, :, 64:128]
         for u in range(2, len(SPANS)):

@@ -81,7 +81,7 @@ def tile_picked_hub_silu_p_kernel(
         load_pass(1, w2, 0)
         load_pass(1, w2, 1)
         nc.sync.dma_start(dst_t[:], dst)
-        raw3 = held([P, TILES, N], F32, "raw3", 4096)
+        raw3 = held([P, TILES, N], F32, "raw3", 8192)
         w3_rows = w3.rearrange("(c t i) m -> t c i m", t=TILES, i=RUN)
         for t in range(TILES):
             nc.sync.dma_start(out=raw3[:, t, :], in_=w3_rows[t])
@@ -143,7 +143,7 @@ def tile_picked_hub_silu_p_kernel(
 
         def empty(copy, which, t, h):
             if h == 0:
-                rows[(which, t)] = held([P, S], F32, "row%d_%d" % (which, t))
+                rows[(which, t)] = held([P, S], F32, "row%d_%d" % (which, t), 4096 - 128 if (which, t) == (1, 0) else None)
             copy(rows[(which, t)][:, h * HALF : (h + 1) * HALF], acc[(which, t, h)][:])
 
         picked = {}
@@ -186,7 +186,7 @@ def tile_picked_hub_silu_p_kernel(
                         multiply(0, z, t, (h,))
                 empty(on_scalar, 0, t, h)
             fetch_sources(t - 1, 0, held([P, HALF], F32, "picked%d_0" % (t - 1), "c0_1_1" if t == 1 else None)[:])
-        fetch_sources(3, 0, held([P, HALF], F32, "picked3_0", 24576)[:])
+        fetch_sources(3, 0, held([P, HALF], F32, "picked3_0", 28672)[:])
 
         cast(on_vector, 1, 0, 0, 2)
         cast(on_vector, 1, 0, 2, 4)
@@ -195,16 +195,16 @@ def tile_picked_hub_silu_p_kernel(
         cast(on_vector, 1, 1, 0, 1)
         cast(on_vector, 1, 1, 1, 2)
         pack(1, 1, 0)
-        cast(on_vector, 1, 1, 2, 4, 0)
+        cast(on_vector, 1, 1, 2, 4, 2048 - 64)
         pack(1, 1, 1)
-        pack(1, 1, 2, 12288)
+        pack(1, 1, 2, 16384)
         for t in range(TILES):
             for h in range(2):
                 for z in range(PASSES):
                     multiply(1, z, t, (h,))
-            empty(on_vector, 1, t, 0)
-            empty(on_vector if t < TILES - 1 else on_scalar, 1, t, 1)
-        late = held([P, TILES, HALF], F32, "late", 13312 - 64)
+            for h in range(2):
+                empty(on_vector if t < TILES - 1 else on_scalar, 1, t, h)
+        late = held([P, TILES, HALF], F32, "late", 17408 - 64)
         for t in range(TILES):
             fetch_sources(t, 1, late[:, t, :])
         grouped3 = held([P, N // P, P * PACK], BF16, "g3", 0)
@@ -258,28 +258,34 @@ def tile_picked_hub_silu_p_kernel(
             copy(result[:], outs[u][:])
             nc.sync.dma_start(out=out[:, lo:hi].rearrange("(m p) r -> p m r", p=P), in_=result[:])
 
-        front = held([P, TILES, HALF], F32, "front", 4096)
+        front = held([P, TILES, HALF], F32, "front", 8192)
         for t in range(TILES - 1):
             add_targets(front[:, t, :], t, 0, HALF)
         for u in range(2):
             lo, hi = SPANS[u]
             sums[u] = front[:, :, lo:hi]
             add_targets(sums[u][:, TILES - 1, :], TILES - 1, lo, hi)
-        codes3 = quantise(grouped3, N // P, "3", 24576)
+        codes3 = quantise(grouped3, N // P, "3", 28672 + 64)
         activate(0)
         activate(1)
-        sums[2] = held([P, TILES, 256], F32, "sums2", 24576 + 1024)[:]
-        sums[3] = held([P, TILES, 128], F32, "sums3", 4096)[:]
-        pair = held([P, TILES, 128], F32, "sums4", 24576 + 1024)
-        sums[4] = pair[:, :, 0:64]
-        sums[5] = pair[:, :, 64:128]
-        for u in range(2, len(SPANS)):
-            if u == 4:
-                for t in range(TILES - 1):
-                    add_targets(pair[:, t, :], t, SPANS[4][0], S)
-            for t in range(TILES) if u < 4 else [TILES - 1]:
+        sums[2] = held([P, TILES, 256], F32, "sums2", 28672 + 1088)[:]
+        sums[3] = held([P, TILES, 128], F32, "sums3", 28672 + 64 - 2048)[:]
+        for u in range(2, 4):
+            for t in range(TILES):
                 add_targets(sums[u][:, t, :], t, *SPANS[u])
             activate(u)
-            for done in {2: (0, 1), 3: (2,), 5: (3, 4, 5)}.get(u, ()):
-                second_layer(done)
-                store(done, on_scalar)
+            second_layer(u - 2)
+            store(u - 2, on_scalar)
+        second_layer(2)
+        store(2, on_scalar)
+        pair = held([P, TILES, 128], F32, "sums4", 28672 + 1088)
+        sums[4] = pair[:, :, 0:64]
+        sums[5] = pair[:, :, 64:128]
+        for t in range(TILES - 1):
+            add_targets(pair[:, t, :], t, SPANS[4][0], S)
+        for u in range(4, 6):
+            add_targets(sums[u][:, TILES - 1, :], TILES - 1, *SPANS[u])
+            activate(u)
+        for u in range(3, 6):
+            second_layer(u)
+            store(u, on_scalar)

@@ -23,6 +23,7 @@ PASSES = K // (P * PACK)
 HALF = 512
 TILES = H // P
 RUN = 4
+E_ON_VECTOR = 6
 SPANS = [(0, 256), (256, 512), (512, 768), (768, 896), (896, 960), (960, 1024)]
 
 
@@ -143,7 +144,7 @@ def tile_picked_hub_silu_p_kernel(
 
         def empty(copy, which, t, h):
             if h == 0:
-                rows[(which, t)] = held([P, S], F32, "row%d_%d" % (which, t), 4096 - 128 if (which, t) == (1, 0) else None)
+                rows[(which, t)] = held([P, S], F32, "row%d_%d" % (which, t), {(1, 0): "g1_1_1", (0, 3): 32768 - 4096}.get((which, t)))
             copy(rows[(which, t)][:, h * HALF : (h + 1) * HALF], acc[(which, t, h)][:])
 
         picked = {}
@@ -170,14 +171,14 @@ def tile_picked_hub_silu_p_kernel(
         xg.append(held([P, S], U32, "xg1"))
         nc.vector.tensor_copy(xg[1][:], xw[1][:].indirect(offs_t[:]))
         cast(on_vector, 0, 1, 0, 1)
+        cast(on_vector, 0, 1, 1, 2)
         pack(0, 1, 0)
         multiply(0, 1, 0)
-        cast(on_scalar, 0, 1, 1, 2)
         pack(0, 1, 1)
         multiply(0, 1, 1)
         cast(on_scalar, 0, 1, 2, 4)
-        empty(on_vector, 0, 0, 0)
         pack(0, 1, 2)
+        empty(on_scalar, 0, 0, 0)
         empty(on_scalar, 0, 0, 1)
         for t in range(1, TILES):
             for h in range(2):
@@ -185,8 +186,8 @@ def tile_picked_hub_silu_p_kernel(
                     for z in range(PASSES):
                         multiply(0, z, t, (h,))
                 empty(on_scalar, 0, t, h)
-            fetch_sources(t - 1, 0, held([P, HALF], F32, "picked%d_0" % (t - 1), "c0_1_1" if t == 1 else None)[:])
-        fetch_sources(3, 0, held([P, HALF], F32, "picked3_0", 28672)[:])
+            fetch_sources(t - 1, 0, held([P, HALF], F32, "picked%d_0" % (t - 1), {1: "c0_1_1", 3: 32768}.get(t))[:])
+        fetch_sources(3, 0, held([P, HALF], F32, "picked3_0")[:])
 
         cast(on_vector, 1, 0, 0, 2)
         cast(on_vector, 1, 0, 2, 4)
@@ -203,10 +204,11 @@ def tile_picked_hub_silu_p_kernel(
                 for z in range(PASSES):
                     multiply(1, z, t, (h,))
             for h in range(2):
-                empty(on_vector if t < TILES - 1 else on_scalar, 1, t, h)
-        late = held([P, TILES, HALF], F32, "late", 17408 - 64)
-        for t in range(TILES):
-            fetch_sources(t, 1, late[:, t, :])
+                empty(on_vector if 2 * t + h < E_ON_VECTOR else on_scalar, 1, t, h)
+        fetch_sources(0, 1, held([P, HALF], F32, "picked0_1", "c1_1_1")[:])
+        late = held([P, TILES - 1, HALF], F32, "late", 17408 - 64)
+        for t in range(1, TILES):
+            fetch_sources(t, 1, late[:, t - 1, :])
         grouped3 = held([P, N // P, P * PACK], BF16, "g3", 0)
         for m in range(N // P):
             nc.gpsimd.tensor_scalar(
@@ -252,9 +254,9 @@ def tile_picked_hub_silu_p_kernel(
                     stop=True,
                 )
 
-        def store(u, copy):
+        def store(u, copy, place=None):
             lo, hi = SPANS[u]
-            result = held([P, N // P, hi - lo], F32, "res%d" % u)
+            result = held([P, N // P, hi - lo], F32, "res%d" % u, place)
             copy(result[:], outs[u][:])
             nc.sync.dma_start(out=out[:, lo:hi].rearrange("(m p) r -> p m r", p=P), in_=result[:])
 
@@ -265,20 +267,20 @@ def tile_picked_hub_silu_p_kernel(
             lo, hi = SPANS[u]
             sums[u] = front[:, :, lo:hi]
             add_targets(sums[u][:, TILES - 1, :], TILES - 1, lo, hi)
-        codes3 = quantise(grouped3, N // P, "3", 28672 + 64)
+        codes3 = quantise(grouped3, N // P, "3", 32768 + 64)
         activate(0)
         activate(1)
-        sums[2] = held([P, TILES, 256], F32, "sums2", 28672 + 1088)[:]
-        sums[3] = held([P, TILES, 128], F32, "sums3", 28672 + 64 - 2048)[:]
+        sums[2] = held([P, TILES, 256], F32, "sums2", 32768 + 1088)[:]
+        sums[3] = held([P, TILES, 128], F32, "sums3", 32768 + 64 - 2048)[:]
         for u in range(2, 4):
             for t in range(TILES):
                 add_targets(sums[u][:, t, :], t, *SPANS[u])
             activate(u)
             second_layer(u - 2)
-            store(u - 2, on_scalar)
+            store(u - 2, on_scalar, 32768 + 1088 + 2048 if u == 2 else 32768 + 64 - 2048)
         second_layer(2)
         store(2, on_scalar)
-        pair = held([P, TILES, 128], F32, "sums4", 28672 + 1088)
+        pair = held([P, TILES, 128], F32, "sums4", 32768 + 1088)
         sums[4] = pair[:, :, 0:64]
         sums[5] = pair[:, :, 64:128]
         for t in range(TILES - 1):

@@ -144,7 +144,7 @@ def tile_picked_hub_silu_p_kernel(
 
         def empty(copy, which, t, h):
             if h == 0:
-                rows[(which, t)] = held([P, S], F32, "row%d_%d" % (which, t), {(1, 0): "g1_1_1", (0, 3): 32768 - 4096}.get((which, t)))
+                rows[(which, t)] = held([P, S], F32, "row%d_%d" % (which, t), {(1, 0): "g1_1_1", (0, 2): "g1_0_0", (0, 3): 32768 - 4096}.get((which, t)))
             copy(rows[(which, t)][:, h * HALF : (h + 1) * HALF], acc[(which, t, h)][:])
 
         picked = {}
@@ -180,19 +180,19 @@ def tile_picked_hub_silu_p_kernel(
         pack(0, 1, 2)
         empty(on_scalar, 0, 0, 0)
         empty(on_scalar, 0, 0, 1)
+        cast(on_vector, 1, 0, 0, 2)
+        cast(on_vector, 1, 0, 2, 4)
+        pack(1, 0, 0)
+        pack(1, 0, 2)
         for t in range(1, TILES):
             for h in range(2):
                 if t > 1:
                     for z in range(PASSES):
                         multiply(0, z, t, (h,))
-                empty(on_scalar, 0, t, h)
-            fetch_sources(t - 1, 0, held([P, HALF], F32, "picked%d_0" % (t - 1), {1: "c0_1_1", 3: 32768}.get(t))[:])
-        fetch_sources(3, 0, held([P, HALF], F32, "picked3_0")[:])
+                empty(on_vector if (t, h) == (2, 1) else on_scalar, 0, t, h)
+            fetch_sources(t - 1, 0, held([P, HALF], F32, "picked%d_0" % (t - 1), {1: "c0_1_1", 3: 40960}.get(t))[:])
+        fetch_sources(3, 0, held([P, HALF], F32, "picked3_0", 32768)[:])
 
-        cast(on_vector, 1, 0, 0, 2)
-        cast(on_vector, 1, 0, 2, 4)
-        pack(1, 0, 0)
-        pack(1, 0, 2)
         cast(on_vector, 1, 1, 0, 1)
         cast(on_vector, 1, 1, 1, 2)
         pack(1, 1, 0)
@@ -267,7 +267,7 @@ def tile_picked_hub_silu_p_kernel(
             lo, hi = SPANS[u]
             sums[u] = front[:, :, lo:hi]
             add_targets(sums[u][:, TILES - 1, :], TILES - 1, lo, hi)
-        codes3 = quantise(grouped3, N // P, "3", 32768 + 64)
+        codes3 = quantise(grouped3, N // P, "3", 40960)
         activate(0)
         activate(1)
         sums[2] = held([P, TILES, 256], F32, "sums2", 32768 + 1088)[:]

@@ -23,7 +23,7 @@ PASSES = K // (P * PACK)
 HALF = 512
 TILES = H // P
 RUN = 4
-E_ON_VECTOR = 6
+E_ON_VECTOR = 5
 SPANS = [(0, 256), (256, 512), (512, 768), (768, 896), (896, 960), (960, 1024)]
 
 

from contextlib import ExitStack

import concourse.mybir as mybir

K, T, S, H, N = 1024, 2048, 1024, 512, 256
FLOPS = 2 * (2 * K * H * S + H * N * S)

F32 = mybir.dt.float32
BF16 = mybir.dt.bfloat16
I32 = mybir.dt.int32
U32 = mybir.dt.uint32
U16 = mybir.dt.uint16
U8 = mybir.dt.uint8
FP8X4 = mybir.dt.float8_e4m3fn_x4
COPY = mybir.ActivationFunctionType.Copy
SILU = mybir.ActivationFunctionType.Silu
ADD = mybir.AluOpType.add
MULT = mybir.AluOpType.mult

P = 128
PACK = 4
PASSES = K // (P * PACK)
HALF = 512
TILES = H // P
RUN = 4
E_ON_VECTOR = 5
SPANS = [(0, 256), (256, 512), (512, 768), (768, 896), (896, 960), (960, 1024)]


def tile_picked_hub_silu_p_kernel(
    tc, x_words, x_scales, w1, w2, w3, offs, src, dst, out
):
    nc = tc.nc
    with ExitStack() as ctx:
        keep = ctx.enter_context(tc.tile_pool(name="keep", bufs=1))
        laid = ctx.enter_context(tc.tile_pool(name="laid", bufs=1))
        psum = ctx.enter_context(tc.psum_pool(name="psum", bufs=1))

        def held(shape, dtype, name, tag=None):
            if isinstance(tag, int):
                return laid.tile(shape, dtype, name=name, tag=name, align_bytes=64, offset=tag)
            return keep.tile(shape, dtype, name=name, tag=tag or name, align_bytes=64)

        def bank(b, shape, name):
            return psum.tile(shape, F32, name=name, tag="bank%d" % b)

        def entries(lst, lo, hi):
            return lst[:, lo // 16 : hi // 16]

        offs_t = held([P, S // 16], U16, "offs_t")
        src_t = held([P, S // 16], U16, "src_t")
        dst_t = held([P, S // 16], U16, "dst_t")
        xw = [held([P, T], U32, "xw0"), held([P, T], U32, "xw1")]
        xs = held([P, T], U8, "xs")

        def load_words(z, lo=0, hi=T):
            nc.sync.dma_start(
                out=xw[z][:, lo:hi].bitcast(I32),
                in_=x_words[z].rearrange("p n t -> p (n t)").bitcast(I32)[:, lo:hi],
            )

        raw = {}

        def load_pass(which, w, z):
            raw[(which, z)] = held([P, PACK, H], F32, "raw%d_%d" % (which, z))
            rows = w[z * P * PACK : (z + 1) * P * PACK, :]
            nc.sync.dma_start(out=raw[(which, z)][:], in_=rows.rearrange("(p j) c -> p j c", j=PACK))

        nc.vector.memset(xs[:].bitcast(I32), 0)
        nc.sync.dma_start(offs_t[:], offs)
        load_words(0, 0, T // 4)
        for q in range(4):
            nc.sync.dma_start(
                out=xs[32 * q : 32 * q + 4 * PASSES, :].bitcast(I32),
                in_=x_scales[:, 4 * q : 4 * q + 4, :].bitcast(I32),
            )
        load_words(0, T // 4, T)
        load_pass(0, w1, 0)
        load_words(1)
        load_pass(0, w1, 1)
        nc.sync.dma_start(src_t[:], src)
        load_pass(1, w2, 0)
        load_pass(1, w2, 1)
        nc.sync.dma_start(dst_t[:], dst)
        raw3 = held([P, TILES, N], F32, "raw3", 8192)
        w3_rows = w3.rearrange("(c t i) m -> t c i m", t=TILES, i=RUN)
        for t in range(TILES):
            nc.sync.dma_start(out=raw3[:, t, :], in_=w3_rows[t])

        warm = held([P, 16], F32, "warm")
        nc.vector.memset(warm[:, 0:8], 0.0)
        nc.scalar.activation(warm[:, 8:9], warm[:, 0:1], SILU)

        on_scalar = nc.scalar.copy
        on_vector = nc.vector.tensor_copy

        def quantise(grouped, count, name, tag=None):
            words = held([P, count, P], U32, "c" + name, tag)
            scales = held([P, count, P], U8, "s" + name)
            nc.vector.quantize_mx(
                out=words[:].rearrange("p a c -> p (a c)").bitcast(FP8X4),
                scales=scales[:].rearrange("p a c -> p (a c)"),
                in_=grouped[:].rearrange("p a c -> p (a c)"),
            )
            return words, scales

        woven = {}
        codes = {}

        def cast(copy, which, z, t0, t1, tag=None):
            grouped = held([P, t1 - t0, P * PACK], BF16, "g%d_%d_%d" % (which, z, t0), tag)
            copy(
                grouped[:].rearrange("p t (c i j) -> p t c j i", i=RUN, j=PACK),
                raw[(which, z)][:].rearrange("p j (c t i) -> p t c j i", t=TILES, i=RUN)[:, t0:t1],
            )
            woven[(which, z, t0)] = (grouped, t1 - t0)

        def pack(which, z, t0, tag=None):
            grouped, count = woven[(which, z, t0)]
            words, scales = quantise(grouped, count, "%d_%d_%d" % (which, z, t0), tag)
            for a in range(count):
                codes[(which, z, t0 + a)] = (words[:, a, :], scales[:, a, :])

        xg = [held([P, S], U32, "xg0")]
        xsg = held([P, S], U8, "xsg")
        acc = {}
        rows = {}

        def multiply(which, z, t, halves=(0, 1)):
            words, scales = codes[(which, z, t)]
            for h in halves:
                if z == 0:
                    acc[(which, t, h)] = bank(4 * which + 2 * (t % 2) + h, [P, HALF], "acc%d_%d_%d" % (which, t, h))
                cols = slice(h * HALF, (h + 1) * HALF)
                nc.tensor.matmul_mx(
                    out=acc[(which, t, h)][:],
                    lhsT=words.bitcast(FP8X4),
                    lhsT_scale=scales,
                    rhs=xg[z][:, cols].bitcast(FP8X4),
                    rhs_scale=xsg[4 * z : P, cols],
                    start=(z == 0),
                    stop=(z == PASSES - 1),
                )

        def empty(copy, which, t, h):
            if h == 0:
                rows[(which, t)] = held([P, S], F32, "row%d_%d" % (which, t), {(1, 0): "g1_1_1", (0, 2): "g1_0_0", (0, 3): 32768 - 4096}.get((which, t)))
            copy(rows[(which, t)][:, h * HALF : (h + 1) * HALF], acc[(which, t, h)][:])

        picked = {}

        def fetch_sources(t, h, into=None):
            if into is None:
                into = held([P, HALF], F32, "picked%d_%d" % (t, h))[:]
            picked[(t, h)] = into
            nc.scalar.activation(into, rows[(0, t)][:].indirect(entries(src_t, h * HALF, (h + 1) * HALF)), COPY)

        def sources(t, lo, hi):
            return picked[(t, lo // HALF)][:, lo % HALF : lo % HALF + hi - lo]

        nc.vector.tensor_copy(xsg[:], xs[:].indirect(offs_t[:]))
        nc.vector.tensor_copy(xg[0][:], xw[0][:].indirect(offs_t[:]))
        cast(on_scalar, 0, 0, 0, 2)
        cast(on_scalar, 0, 0, 2, 3)
        cast(on_vector, 0, 0, 3, 4)
        pack(0, 0, 0)
        pack(0, 0, 2)
        pack(0, 0, 3)
        for t in range(2):
            multiply(0, 0, t)
        xg.append(held([P, S], U32, "xg1"))
        nc.vector.tensor_copy(xg[1][:], xw[1][:].indirect(offs_t[:]))
        cast(on_vector, 0, 1, 0, 1)
        cast(on_vector, 0, 1, 1, 2)
        pack(0, 1, 0)
        multiply(0, 1, 0)
        pack(0, 1, 1)
        multiply(0, 1, 1)
        cast(on_scalar, 0, 1, 2, 4)
        pack(0, 1, 2)
        empty(on_scalar, 0, 0, 0)
        empty(on_scalar, 0, 0, 1)
        cast(on_vector, 1, 0, 0, 2)
        cast(on_vector, 1, 0, 2, 4)
        pack(1, 0, 0)
        pack(1, 0, 2)
        for t in range(1, TILES):
            for h in range(2):
                if t > 1:
                    for z in range(PASSES):
                        multiply(0, z, t, (h,))
                empty(on_vector if (t, h) == (2, 1) else on_scalar, 0, t, h)
            fetch_sources(t - 1, 0, held([P, HALF], F32, "picked%d_0" % (t - 1), {1: "c0_1_1", 3: 40960}.get(t))[:])
        fetch_sources(3, 0, held([P, HALF], F32, "picked3_0", 32768)[:])

        cast(on_vector, 1, 1, 0, 1)
        cast(on_vector, 1, 1, 1, 2)
        pack(1, 1, 0)
        cast(on_vector, 1, 1, 2, 4, 2048 - 64)
        pack(1, 1, 1)
        pack(1, 1, 2, 16384)
        for t in range(TILES):
            for h in range(2):
                for z in range(PASSES):
                    multiply(1, z, t, (h,))
            for h in range(2):
                empty(on_vector if 2 * t + h < E_ON_VECTOR else on_scalar, 1, t, h)
        fetch_sources(0, 1, held([P, HALF], F32, "picked0_1", "c1_1_1")[:])
        late = held([P, TILES - 1, HALF], F32, "late", 17408 - 64)
        for t in range(1, TILES):
            fetch_sources(t, 1, late[:, t - 1, :])
        grouped3 = held([P, N // P, P * PACK], BF16, "g3", 0)
        for m in range(N // P):
            nc.gpsimd.tensor_scalar(
                grouped3[:, m, :].rearrange("p (c j) -> p c j", j=PACK),
                raw3[:, :, m * P : (m + 1) * P].rearrange("p j c -> p c j"),
                1.0,
                0.0,
                MULT,
                ADD,
            )

        sums = {}
        z_in = {}

        def add_targets(into, t, lo, hi):
            nc.vector.tensor_tensor(into, rows[(1, t)][:].indirect(entries(dst_t, lo, hi)), sources(t, lo, hi), ADD)

        def activate(u):
            lo, hi = SPANS[u]
            z_in[u] = held([P, (hi - lo) * PACK], BF16, "z_in%d" % u)
            nc.scalar.activation(
                z_in[u][:].rearrange("p (c i t) -> p c t i", i=RUN, t=TILES),
                sums[u].rearrange("p t (c i) -> p c t i", i=RUN),
                SILU,
            )

        outs = {}

        def second_layer(u):
            lo, hi = SPANS[u]
            words = held([P, hi - lo], U32, "zc%d" % u)
            scales = held([P, hi - lo], U8, "zs%d" % u)
            nc.vector.quantize_mx(out=words[:].bitcast(FP8X4), scales=scales[:], in_=z_in[u][:])
            outs[u] = bank(u, [P, N // P, hi - lo], "oacc%d" % u)
            for m in range(N // P):
                nc.tensor.matmul_mx(
                    out=outs[u][:, m, :],
                    lhsT=codes3[0][:, m, :].bitcast(FP8X4),
                    lhsT_scale=codes3[1][:, m, :],
                    rhs=words[:].bitcast(FP8X4),
                    rhs_scale=scales[:],
                    start=True,
                    stop=True,
                )

        def store(u, copy, place=None):
            lo, hi = SPANS[u]
            result = held([P, N // P, hi - lo], F32, "res%d" % u, place)
            copy(result[:], outs[u][:])
            nc.sync.dma_start(out=out[:, lo:hi].rearrange("(m p) r -> p m r", p=P), in_=result[:])

        front = held([P, TILES, HALF], F32, "front", 8192)
        for t in range(TILES - 1):
            add_targets(front[:, t, :], t, 0, HALF)
        for u in range(2):
            lo, hi = SPANS[u]
            sums[u] = front[:, :, lo:hi]
            add_targets(sums[u][:, TILES - 1, :], TILES - 1, lo, hi)
        codes3 = quantise(grouped3, N // P, "3", 40960)
        activate(0)
        activate(1)
        sums[2] = held([P, TILES, 256], F32, "sums2", 32768 + 1088)[:]
        sums[3] = held([P, TILES, 128], F32, "sums3", 32768 + 64 - 2048)[:]
        for u in range(2, 4):
            for t in range(TILES):
                add_targets(sums[u][:, t, :], t, *SPANS[u])
            activate(u)
            second_layer(u - 2)
            store(u - 2, on_scalar, 32768 + 1088 + 2048 if u == 2 else 32768 + 64 - 2048)
        second_layer(2)
        store(2, on_scalar)
        pair = held([P, TILES, 128], F32, "sums4", 32768 + 1088)
        sums[4] = pair[:, :, 0:64]
        sums[5] = pair[:, :, 64:128]
        for t in range(TILES - 1):
            add_targets(pair[:, t, :], t, SPANS[4][0], S)
        for u in range(4, 6):
            add_targets(sums[u][:, TILES - 1, :], TILES - 1, *SPANS[u])
            activate(u)
        for u in range(3, 6):
            second_layer(u)
            store(u, on_scalar)
